import numpy as np
import ml_dtypes


def mxq(x, axis, fmt="e4m3"):
    dtype, down = {"e4m3": (ml_dtypes.float8_e4m3fn, 7), "e5m2": (ml_dtypes.float8_e5m2, 14)}[fmt]
    v = np.moveaxis(np.asarray(x, np.float32).astype(ml_dtypes.bfloat16).astype(np.float64), axis, -1)
    blocks = v.reshape(v.shape[:-1] + (-1, 32))
    amax = np.abs(blocks).max(-1, keepdims=True)
    byte = np.maximum(np.where(amax > 0, np.frexp(amax)[1] - 1 + 127, 0) - down, 1)
    scale = np.exp2(byte - 127.0)
    codes = (blocks / scale).astype(np.float32).astype(dtype).astype(np.float64)
    return np.moveaxis((codes * scale).reshape(v.shape), -1, axis)


WIDE = False


def mx_kscale(k):
    if not WIDE:
        return np.ones(k)
    levels = np.array([10, -10, 5, -5, 0])
    if k % 512:
        return np.exp2(np.random.permutation(np.resize(levels, k // 32))).repeat(32)
    a = np.empty((k // 512, 16))
    for p in range(k // 512):
        a[p, :8] = np.random.permutation(np.resize(levels, 8))
        for g in range(8):
            far = levels[np.abs(levels - a[p, g]) >= 10]
            a[p, g + 8] = far[np.random.randint(len(far))]
    return np.exp2(a.ravel()).repeat(32)


def f64(x):
    return np.asarray(x).astype(np.float64)


def striped(idx):
    return np.tile(idx.reshape(-1, 16).T, (8, 1)).astype(np.uint16)


def unstriped(offs):
    return offs[:16].T.reshape(-1).astype(np.int64)


E2M1 = np.array([0.0, 0.5, 1.0, 1.5, 2.0, 3.0, 4.0, 6.0, -0.0, -0.5, -1.0, -1.5, -2.0, -3.0, -4.0, -6.0])


def pack_weight(w, fmt):
    k, n = w.shape
    w = f64(np.asarray(w, np.float32).astype(ml_dtypes.bfloat16)).reshape(k // 32, 32, n)
    amax = np.abs(w).max(1)
    if fmt == "e4m3":
        byte = np.frexp(amax)[1] - 1 + 127 - 7
    else:
        mant, ex = np.frexp(amax / 6.0)
        byte = np.where(mant > 0.5, ex, ex - 1) + 127
    byte = np.clip(np.where(amax > 0, byte, 1), 1, 254)
    scaled = (w * np.exp2(127.0 - byte)[:, None, :]).reshape(k, n).astype(np.float32)
    by_word = np.ascontiguousarray(scaled.reshape(k // 512, 128, 4, n).transpose(0, 1, 3, 2))
    if fmt == "e4m3":
        words = by_word.astype(ml_dtypes.float8_e4m3fn).view(np.uint8)
    else:
        c = by_word.astype(ml_dtypes.float4_e2m1fn).view(np.uint8) & 0xF
        words = (c[..., 0::2] | (c[..., 1::2] << 4)).reshape(k // 512, 128, 2 * n)
    return np.ascontiguousarray(words), np.ascontiguousarray(byte.astype(np.uint8).reshape(k // 512, 16, n))


def unpack_weight(words, scales, fmt):
    g, _, n = scales.shape
    words = np.ascontiguousarray(words).reshape(g, 128, n, -1)
    if fmt == "e4m3":
        vals = words.view(ml_dtypes.float8_e4m3fn).astype(np.float64)
    else:
        nib = np.empty((g, 128, n, 4), np.uint8)
        nib[..., 0::2] = words & 0xF
        nib[..., 1::2] = words >> 4
        vals = E2M1[nib]
    vals = vals * np.repeat(np.exp2(scales.astype(np.float64) - 127.0), 8, axis=1)[..., None]
    return vals.transpose(0, 1, 3, 2).reshape(g * 512, n)


def gelu(v):
    return 0.5 * v * (1.0 + np.tanh(np.sqrt(2.0 / np.pi) * (v + 0.044715 * v**3)))


def striped8(idx):
    return np.concatenate([v.reshape(-1, 16).T for v in idx]).astype(np.uint16)


def unstriped8(offs):
    return np.stack([offs[16 * g:16 * g + 16].T.reshape(-1) for g in range(8)]).astype(np.int64)


def runs(v, idx8):
    k = np.arange(v.shape[0])
    return v[k[:, None], idx8[k % 512 // 64]]


def put_heads(h, wgs, idx8, t2):
    r = np.arange(h.shape[0])
    page = np.zeros((h.shape[0], t2))
    page[r[:, None], idx8[r % 512 // 64]] = wgs[r // 4 % 128] * h
    return page


K, H, N, T, S, T2 = 1024, 1024, 512, 2048, 1024, 2048

def setup_inputs():
    n = np.random.standard_normal
    s = mx_kscale(K)[:, None]
    u = mx_kscale(H)[:, None]
    tab_words, tab_scales = pack_weight(n((K, T)) * s, "e4m3")
    wa_words, wa_scales = pack_weight(n((K, H)) / np.sqrt(K) / s * u.T, "e2m1")
    wb = (n((K, H)) / np.sqrt(K) / s).astype(np.float32)
    wc_words, wc_scales = pack_weight(1.5 * n((H, N)) / np.sqrt(H) / u, "e4m3")
    backdrop = (0.7 * n((N, S))).astype(np.float32)
    offs = striped8(np.stack([np.random.permutation(T)[:S] for _ in range(8)]))
    offs2 = striped8(np.stack([np.random.permutation(T2)[:S] for _ in range(8)]))
    wgo = np.repeat(np.random.uniform(0.5, 2.0, (8, S)), 16, axis=0).astype(np.float32)
    return {"tab_words": tab_words, "tab_scales": tab_scales, "offs": offs,
            "wa_words": wa_words, "wa_scales": wa_scales, "wb": wb,
            "wc_words": wc_words, "wc_scales": wc_scales,
            "backdrop": backdrop, "wgo": wgo, "offs2": offs2}

def reference(tab_words, tab_scales, offs, wa_words, wa_scales, wb, wc_words, wc_scales,
              backdrop, wgo, offs2):
    v = runs(unpack_weight(tab_words, tab_scales, "e4m3"), unstriped8(offs))
    a = unpack_weight(wa_words, wa_scales, "e2m1").T @ v
    b = mxq(f64(wb), 0, "e4m3").T @ v
    h = a / (1.0 + np.abs(b))
    hq = mxq(h, 0, "e4m3")
    y = (unpack_weight(wc_words, wc_scales, "e4m3").T @ hq) - f64(backdrop)
    out = put_heads(y, f64(wgo), unstriped8(offs2), T2)
    return out

@@ -1,0 +1,257 @@
+from contextlib import ExitStack
+
+import concourse.mybir as mybir
+
+K, H, N, T, S, T2 = 1024, 1024, 512, 2048, 1024, 2048
+FLOPS = 2 * K * H * S * 2 + 2 * H * N * S
+
+F32 = mybir.dt.float32
+BF16 = mybir.dt.bfloat16
+I32 = mybir.dt.int32
+U32 = mybir.dt.uint32
+U16 = mybir.dt.uint16
+U8 = mybir.dt.uint8
+FP8X4 = mybir.dt.float8_e4m3fn_x4
+FP4X4 = mybir.dt.float4_e2m1fn_x4
+ACT = mybir.ActivationFunctionType
+ALU = mybir.AluOpType
+
+P = 128
+PACK = 4
+KP = P * PACK
+PASSES = K // KP
+BLOCKS = H // KP
+CH = 128
+CHUNKS = S // CH
+HALF = S // 2
+AHEAD = 4
+
+
+def tile_list_silhouette_atlas_features_kernel(
+    tc, tab_words, tab_scales, offs, wa_words, wa_scales, wb, wc_words, wc_scales, backdrop, wgo, offs2, out
+):
+    nc = tc.nc
+    with ExitStack() as ctx:
+        lists = ctx.enter_context(tc.tile_pool(name="lists", bufs=1))
+        keep = ctx.enter_context(tc.tile_pool(name="keep", bufs=1))
+        ring = ctx.enter_context(tc.tile_pool(name="ring", bufs=3))
+        psum_ab = ctx.enter_context(tc.psum_pool(name="psum_ab", bufs=3))
+        psum_y = ctx.enter_context(tc.psum_pool(name="psum_y", bufs=2))
+
+        pick = lists.tile([P, S // 16], U16, name="pick")
+        place = lists.tile([P, S // 16], U16, name="place")
+
+        WS = H + N
+        ROW = S + WS
+        ts_raw = keep.tile([P, T], U8, name="ts_raw", tag="s0", align_bytes=64)
+        ws_raw = keep.tile([P, WS], U8, name="ws_raw", tag="s1", align_bytes=64)
+        plane = keep.tile([P, PASSES * ROW], U8, name="plane", align_bytes=64)
+        nc.vector.memset(ts_raw[:].bitcast(I32), 0)
+        nc.vector.memset(ws_raw[:].bitcast(I32), 0)
+        warm_in = keep.tile([P, 1], F32, name="warm_in", tag="tab1", align_bytes=64)
+        warm_out = keep.tile([P, 1], F32, name="warm_out", tag="w00", align_bytes=64)
+        warm_bias = keep.tile([P, 1], F32, name="warm_bias", tag="w10", align_bytes=64)
+        nc.vector.memset(warm_in[:], 1.0)
+        nc.vector.memset(warm_bias[:], 1.0)
+        nc.scalar.activation(warm_out[:], warm_in[:], ACT.Abs_reciprocal_sqrt, bias=warm_bias[:])
+        nc.vector.memset(plane[:].bitcast(I32), 0)
+
+        nc.sync.dma_start(pick[:], offs)
+        nc.sync.dma_start(place[:], offs2)
+        tab = [keep.tile([P, T], I32, name=f"tab{a}", tag=f"tab{a}", align_bytes=64) for a in range(PASSES)]
+        wb_raw = {}
+        WB = PACK * KP
+
+        def load_tab(a):
+            nc.sync.dma_start(tab[a][:], tab_words[a].rearrange("p t i -> p (t i)").bitcast(I32))
+
+        def load_wb(a, b, room):
+            wb_raw[a, b] = room.rearrange("p (j c) -> p j c", j=PACK)
+            rows = wb[a * KP : (a + 1) * KP, b * KP : (b + 1) * KP]
+            nc.sync.dma_start(wb_raw[a, b], rows.rearrange("(p j) c -> p j c", j=PACK))
+
+        load_tab(0)
+        nc.sync.dma_start(ts_raw[0:P:4, :].bitcast(I32), tab_scales.bitcast(I32).rearrange("a q t -> q a t"))
+        nc.sync.dma_start(ws_raw[0:P:4, 0:H].bitcast(I32), wa_scales.bitcast(I32).rearrange("a q c -> q a c"))
+        nc.sync.dma_start(ws_raw[0:P:4, H:WS].bitcast(I32), wc_scales.bitcast(I32).rearrange("a q c -> q a c"))
+        room00 = keep.tile([P, WB], F32, name="room00", tag="w00", align_bytes=64)
+        room10 = keep.tile([P, WB], F32, name="room10", tag="w10", align_bytes=64)
+        load_wb(0, 0, room00[:])
+        load_tab(1)
+        load_wb(1, 0, room10[:])
+
+        ts_got = keep.tile([P, S], U8, name="ts_got", tag="s2", align_bytes=64)
+        nc.vector.tensor_copy(ts_got[:], ts_raw[:].indirect(pick[:]))
+        staged = keep.tile([P, ROW], U8, name="staged", align_bytes=64)
+        nc.vector.tensor_copy(staged[:, 0:S].bitcast(I32), ts_got[:].bitcast(I32))
+        nc.vector.tensor_copy(
+            staged[:, S:ROW].rearrange("p (g t m) -> p g t m", t=PACK, m=P),
+            ws_raw[:].rearrange("p (g m t) -> p g t m", t=PACK, m=P),
+        )
+        for d in range(4):
+            nc.sync.dma_start(
+                plane[32 * d : 32 * d + 4, :].bitcast(I32).rearrange("p (a c) -> p a c", a=PASSES),
+                staged[32 * d : 32 * d + 32 : 4, :].bitcast(I32),
+            )
+        wa_raw = keep.tile([P, H], I32, name="wa_raw", tag="s1", align_bytes=64)
+        nc.sync.dma_start(
+            wa_raw[:].rearrange("p (a c) -> p a c", a=PASSES), wa_words.bitcast(I32).rearrange("a p c -> p a c")
+        )
+        bd_rows = backdrop.rearrange("(p i) j -> p i j", i=PACK)
+
+        got = {}
+
+        def gather_words(a, half, tag):
+            got[a, half] = keep.tile([P, HALF], U32, name=f"got{a}{half}", tag=tag, align_bytes=64)
+            cols = slice(half * HALF // 16, (half + 1) * HALF // 16)
+            nc.vector.tensor_copy(got[a, half][:], tab[a][:].bitcast(U32).indirect(pick[:, cols]))
+
+        wb_codes, wb_scales = {}, {}
+
+        def quantize_wb(a, b, on_scalar):
+            rounded = keep.tile([P, KP * PACK], BF16, name=f"wb_bf{a}{b}", tag=f"bf{a}{b}", align_bytes=64)
+            dst = rounded[:].rearrange("p (t m j) -> p m t j", t=PACK, j=PACK)
+            src = wb_raw[a, b].rearrange("p j (m t) -> p m t j", t=PACK)
+            if on_scalar:
+                nc.scalar.copy(dst, src)
+            else:
+                nc.vector.tensor_copy(dst, src)
+            wb_codes[a, b] = keep.tile([P, KP], U32, name=f"wb_codes{a}{b}", align_bytes=64)
+            wb_scales[a, b] = keep.tile([P, KP], U8, name=f"wb_scales{a}{b}", align_bytes=64)
+            nc.vector.quantize_mx(out=wb_codes[a, b][:].bitcast(FP8X4), scales=wb_scales[a, b][:], in_=rounded[:])
+
+        gather_words(0, 0, "g00")
+        quantize_wb(0, 0, True)
+        wave3 = keep.tile([P, PASSES * WB], F32, name="wave3", tag="w00", align_bytes=64)
+        load_wb(0, 1, wave3[:, 0:WB])
+        load_wb(1, 1, wave3[:, WB : 2 * WB])
+        wc_raw = keep.tile([P, BLOCKS, N], I32, name="wc_raw", tag="bf00", align_bytes=64)
+        nc.sync.dma_start(
+            wc_raw[:], wc_words.rearrange("a p c i -> a p (c i)").bitcast(I32).rearrange("a p c -> p a c")
+        )
+        gather_words(1, 0, "g10")
+        quantize_wb(1, 0, True)
+        wave4 = keep.tile([P, (PACK + 1) * S], F32, name="wave4", tag="w10", align_bytes=64)
+        bd = [
+            wave4[:, q * PACK * HALF : (q + 1) * PACK * HALF].rearrange("p (i j) -> p i j", i=PACK) for q in range(2)
+        ]
+        weight = wave4[:, PACK * S : (PACK + 1) * S]
+        nc.sync.dma_start(bd[0], bd_rows[:, :, 0:HALF])
+        nc.sync.dma_start(weight, wgo)
+        nc.sync.dma_start(bd[1], bd_rows[:, :, HALF:S])
+        wa_ord = keep.tile([P, PASSES * 2 * H], U8, name="wa_ord", align_bytes=64)
+        nc.vector.tensor_copy(
+            wa_ord[:].bitcast(U16).rearrange("p (g t m) -> p g t m", g=PASSES * BLOCKS, t=PACK),
+            wa_raw[:].bitcast(U16).rearrange("p (g m t) -> p g t m", g=PASSES * BLOCKS, t=PACK),
+        )
+
+        h_codes, h_scales = {}, {}
+
+        def unit(b, c):
+            half, col = divmod(c * CH, HALF)
+            bank_a = psum_ab.tile([P, PACK, CH], F32, name="bank_a")
+            bank_b = psum_ab.tile([P, PACK, CH], F32, name="bank_b")
+            for t in range(PACK):
+                for a in range(PASSES):
+                    nc.tensor.matmul_mx(
+                        out=bank_b[:, t, :],
+                        lhsT=wb_codes[a, b][:, t * P : (t + 1) * P].bitcast(FP8X4),
+                        lhsT_scale=wb_scales[a, b][:, t * P : (t + 1) * P],
+                        rhs=got[a, half][:, col : col + CH].bitcast(FP8X4),
+                        rhs_scale=plane[:, a * ROW + c * CH : a * ROW + (c + 1) * CH],
+                        start=(a == 0),
+                        stop=(a == PASSES - 1),
+                    )
+            for t in range(PACK):
+                for a in range(PASSES):
+                    w0 = a * H + b * KP + t * P
+                    s0 = a * ROW + S + b * KP + t * P
+                    nc.tensor.matmul_mx(
+                        out=bank_a[:, t, :],
+                        lhsT=wa_ord[:, 2 * w0 : 2 * (w0 + P)].bitcast(FP4X4),
+                        lhsT_scale=plane[:, s0 : s0 + P],
+                        rhs=got[a, half][:, col : col + CH].bitcast(FP8X4),
+                        rhs_scale=plane[:, a * ROW + c * CH : a * ROW + (c + 1) * CH],
+                        start=(a == 0),
+                        stop=(a == PASSES - 1),
+                    )
+            size = ring.tile([P, CH * PACK], F32, name="size")
+            root = ring.tile([P, CH * PACK], F32, name="root")
+            recip = ring.tile([P, CH * PACK], F32, name="recip")
+            nc.scalar.activation(
+                size[:].rearrange("p (n t) -> p n t", t=PACK), bank_b[:].rearrange("p t n -> p n t"), ACT.Abs
+            )
+            nc.scalar.activation(root[:], size[:], ACT.Abs_reciprocal_sqrt, bias=1.0)
+            nc.scalar.activation(recip[:], root[:], ACT.Square)
+            h_bf = ring.tile([P, CH * PACK], BF16, name="h_bf", align_bytes=64)
+            nc.vector.tensor_tensor(
+                h_bf[:].rearrange("p (n t) -> p n t", t=PACK),
+                bank_a[:].rearrange("p t n -> p n t"),
+                recip[:].rearrange("p (n t) -> p n t", t=PACK),
+                ALU.mult,
+            )
+            h_codes[b, c] = keep.tile([P, CH], U32, name=f"h_codes{b}{c}", align_bytes=64)
+            h_scales[b, c] = keep.tile([P, CH], U8, name=f"h_scales{b}{c}", align_bytes=64)
+            nc.vector.quantize_mx(out=h_codes[b, c][:].bitcast(FP8X4), scales=h_scales[b, c][:], in_=h_bf[:])
+
+        wc_ord = keep.tile([P, BLOCKS * N], U32, name="wc_ord", align_bytes=64)
+        diff = keep.tile([P, PACK, S], F32, name="diff")
+
+        def second_stage(c):
+            bank_y = psum_y.tile([P, PACK, CH], F32, name="bank_y")
+            for i in range(PACK):
+                for b in range(BLOCKS):
+                    s0 = b * ROW + S + H + i * P
+                    nc.tensor.matmul_mx(
+                        out=bank_y[:, i, :],
+                        lhsT=wc_ord[:, b * N + i * P : b * N + (i + 1) * P].bitcast(FP8X4),
+                        lhsT_scale=plane[:, s0 : s0 + P],
+                        rhs=h_codes[b, c][:].bitcast(FP8X4),
+                        rhs_scale=h_scales[b, c][:],
+                        start=(b == 0),
+                        stop=(b == BLOCKS - 1),
+                    )
+            q, col = divmod(c * CH, HALF)
+            nc.vector.tensor_tensor(
+                diff[:, :, c * CH : (c + 1) * CH], bank_y[:], bd[q][:, :, col : col + CH], ALU.subtract
+            )
+
+        pages = {}
+        out_rows = out.rearrange("(p i) t -> p i t", i=PACK)
+
+        def scatter(i, lo, hi):
+            nc.vector.tensor_tensor(
+                pages[i][:].indirect(place[:, lo // 16 : hi // 16]), diff[:, i, lo:hi], weight[:, lo:hi], ALU.mult
+            )
+            if hi == S:
+                nc.sync.dma_start(out_rows[:, i, :], pages[i][:])
+
+        unit(0, 0)
+        unit(0, 1)
+        quantize_wb(0, 1, True)
+        unit(0, 2)
+        quantize_wb(1, 1, False)
+        unit(0, 3)
+        nc.vector.tensor_copy(
+            wc_ord[:].bitcast(I32).rearrange("p (b i g m) -> p b g i m", b=BLOCKS, i=PACK, m=4),
+            wc_raw[:].rearrange("p b (g m i) -> p b g i m", i=PACK, m=4),
+        )
+        gather_words(0, 1, "bf01")
+        gather_words(1, 1, "bf11")
+        for i in range(2):
+            pages[i] = keep.tile([P, T2], F32, name=f"page{i}", align_bytes=64)
+            nc.vector.memset(pages[i][:].bitcast(I32), 0)
+        for i in range(2, PACK):
+            pages[i] = keep.tile([P, T2], F32, name=f"page{i}", tag=f"tab{i - 2}", align_bytes=64)
+            for lo in range(0, T2, 512):
+                nc.gpsimd.memset(pages[i][:, lo : lo + 512], 0.0)
+        for c in range(CHUNKS):
+            unit(1, c)
+            if c + AHEAD < CHUNKS:
+                unit(0, c + AHEAD)
+            second_stage(c)
+            if c % 2 == 1:
+                for i in range(2):
+                    scatter(i, (c - 1) * CH, (c + 1) * CH)
+        for i in range(2, PACK):
+            scatter(i, 0, S)

@@ -24,7 +24,7 @@ BLOCKS = H // KP
 CH = 128
 CHUNKS = S // CH
 HALF = S // 2
-AHEAD = 4
+AHEAD = 2
 
 
 def tile_list_silhouette_atlas_features_kernel(
@@ -77,8 +77,8 @@ def tile_list_silhouette_atlas_features_kernel(
         room00 = keep.tile([P, WB], F32, name="room00", tag="w00", align_bytes=64)
         room10 = keep.tile([P, WB], F32, name="room10", tag="w10", align_bytes=64)
         load_wb(0, 0, room00[:])
-        load_tab(1)
         load_wb(1, 0, room10[:])
+        load_tab(1)
 
         ts_got = keep.tile([P, S], U8, name="ts_got", tag="s2", align_bytes=64)
         nc.vector.tensor_copy(ts_got[:], ts_raw[:].indirect(pick[:]))
@@ -120,7 +120,7 @@ def tile_list_silhouette_atlas_features_kernel(
             wb_scales[a, b] = keep.tile([P, KP], U8, name=f"wb_scales{a}{b}", align_bytes=64)
             nc.vector.quantize_mx(out=wb_codes[a, b][:].bitcast(FP8X4), scales=wb_scales[a, b][:], in_=rounded[:])
 
-        gather_words(0, 0, "g00")
+        gather_words(0, 0, "s0")
         quantize_wb(0, 0, True)
         wave3 = keep.tile([P, PASSES * WB], F32, name="wave3", tag="w00", align_bytes=64)
         load_wb(0, 1, wave3[:, 0:WB])
@@ -129,8 +129,8 @@ def tile_list_silhouette_atlas_features_kernel(
         nc.sync.dma_start(
             wc_raw[:], wc_words.rearrange("a p c i -> a p (c i)").bitcast(I32).rearrange("a p c -> p a c")
         )
-        gather_words(1, 0, "g10")
         quantize_wb(1, 0, True)
+        gather_words(1, 0, "g10")
         wave4 = keep.tile([P, (PACK + 1) * S], F32, name="wave4", tag="w10", align_bytes=64)
         bd = [
             wave4[:, q * PACK * HALF : (q + 1) * PACK * HALF].rearrange("p (i j) -> p i j", i=PACK) for q in range(2)
@@ -145,7 +145,8 @@ def tile_list_silhouette_atlas_features_kernel(
             wa_raw[:].bitcast(U16).rearrange("p (g m t) -> p g t m", g=PASSES * BLOCKS, t=PACK),
         )
 
-        h_codes, h_scales = {}, {}
+        h_bf, h_codes, h_scales = {}, {}, {}
+        diff = keep.tile([P, PACK, S], F32, name="diff")
 
         def unit(b, c):
             half, col = divmod(c * CH, HALF)
@@ -177,25 +178,33 @@ def tile_list_silhouette_atlas_features_kernel(
                     )
             size = ring.tile([P, CH * PACK], F32, name="size")
             root = ring.tile([P, CH * PACK], F32, name="root")
-            recip = ring.tile([P, CH * PACK], F32, name="recip")
             nc.scalar.activation(
                 size[:].rearrange("p (n t) -> p n t", t=PACK), bank_b[:].rearrange("p t n -> p n t"), ACT.Abs
             )
             nc.scalar.activation(root[:], size[:], ACT.Abs_reciprocal_sqrt, bias=1.0)
-            nc.scalar.activation(recip[:], root[:], ACT.Square)
-            h_bf = ring.tile([P, CH * PACK], BF16, name="h_bf", align_bytes=64)
+            if b == 1 and c > 0:
+                recip = diff[:, :, (c - 1) * CH : c * CH]
+            else:
+                spare = ring.tile([P, PACK, CH], F32, name="spare")
+                recip = spare[:]
+            nc.scalar.activation(recip, root[:].rearrange("p (g x) -> p g x", g=PACK), ACT.Square)
+            if b == 0:
+                h_bf[c] = keep.tile([P, BLOCKS * KP], BF16, name=f"h_bf{c}", align_bytes=64)
             nc.vector.tensor_tensor(
-                h_bf[:].rearrange("p (n t) -> p n t", t=PACK),
-                bank_a[:].rearrange("p t n -> p n t"),
-                recip[:].rearrange("p (n t) -> p n t", t=PACK),
+                h_bf[c][:, b * KP : (b + 1) * KP].rearrange("p (g n t) -> p g n t", g=PACK, t=PACK),
+                bank_a[:].rearrange("p t (g n) -> p g n t", g=PACK),
+                recip.rearrange("p g (n t) -> p g n t", t=PACK),
                 ALU.mult,
             )
-            h_codes[b, c] = keep.tile([P, CH], U32, name=f"h_codes{b}{c}", align_bytes=64)
-            h_scales[b, c] = keep.tile([P, CH], U8, name=f"h_scales{b}{c}", align_bytes=64)
-            nc.vector.quantize_mx(out=h_codes[b, c][:].bitcast(FP8X4), scales=h_scales[b, c][:], in_=h_bf[:])
+
+        def quantize_h(c):
+            h_codes[c] = keep.tile([P, BLOCKS * CH], U32, name=f"h_codes{c}", align_bytes=64)
+            h_scales[c] = keep.tile([P, BLOCKS * CH], U8, name=f"h_scales{c}", align_bytes=64)
+            nc.vector.quantize_mx(out=h_codes[c][:].bitcast(FP8X4), scales=h_scales[c][:], in_=h_bf[c][:])
 
         wc_ord = keep.tile([P, BLOCKS * N], U32, name="wc_ord", align_bytes=64)
-        diff = keep.tile([P, PACK, S], F32, name="diff")
+
+        banks_y = {}
 
         def second_stage(c):
             bank_y = psum_y.tile([P, PACK, CH], F32, name="bank_y")
@@ -206,14 +215,17 @@ def tile_list_silhouette_atlas_features_kernel(
                         out=bank_y[:, i, :],
                         lhsT=wc_ord[:, b * N + i * P : b * N + (i + 1) * P].bitcast(FP8X4),
                         lhsT_scale=plane[:, s0 : s0 + P],
-                        rhs=h_codes[b, c][:].bitcast(FP8X4),
-                        rhs_scale=h_scales[b, c][:],
+                        rhs=h_codes[c][:, b * CH : (b + 1) * CH].bitcast(FP8X4),
+                        rhs_scale=h_scales[c][:, b * CH : (b + 1) * CH],
                         start=(b == 0),
                         stop=(b == BLOCKS - 1),
                     )
+            banks_y[c] = bank_y
+
+        def subtract(c):
             q, col = divmod(c * CH, HALF)
             nc.vector.tensor_tensor(
-                diff[:, :, c * CH : (c + 1) * CH], bank_y[:], bd[q][:, :, col : col + CH], ALU.subtract
+                diff[:, :, c * CH : (c + 1) * CH], banks_y[c][:], bd[q][:, :, col : col + CH], ALU.subtract
             )
 
         pages = {}
@@ -228,30 +240,33 @@ def tile_list_silhouette_atlas_features_kernel(
 
         unit(0, 0)
         unit(0, 1)
-        quantize_wb(0, 1, True)
-        unit(0, 2)
+        quantize_wb(0, 1, False)
         quantize_wb(1, 1, False)
-        unit(0, 3)
+        unit(0, 2)
         nc.vector.tensor_copy(
             wc_ord[:].bitcast(I32).rearrange("p (b i g m) -> p b g i m", b=BLOCKS, i=PACK, m=4),
             wc_raw[:].rearrange("p b (g m i) -> p b g i m", i=PACK, m=4),
         )
         gather_words(0, 1, "bf01")
-        gather_words(1, 1, "bf11")
-        for i in range(2):
-            pages[i] = keep.tile([P, T2], F32, name=f"page{i}", align_bytes=64)
-            nc.vector.memset(pages[i][:].bitcast(I32), 0)
-        for i in range(2, PACK):
-            pages[i] = keep.tile([P, T2], F32, name=f"page{i}", tag=f"tab{i - 2}", align_bytes=64)
+        gather_words(1, 1, "w00")
+        pages[0] = keep.tile([P, T2], F32, name="page0", align_bytes=64)
+        nc.vector.memset(pages[0][:].bitcast(I32), 0)
+        for i, tag in ((1, "bf11"), (2, "tab0"), (3, "tab1")):
+            pages[i] = keep.tile([P, T2], F32, name=f"page{i}", tag=tag, align_bytes=64)
             for lo in range(0, T2, 512):
                 nc.gpsimd.memset(pages[i][:, lo : lo + 512], 0.0)
-        for c in range(CHUNKS):
-            unit(1, c)
-            if c + AHEAD < CHUNKS:
-                unit(0, c + AHEAD)
-            second_stage(c)
-            if c % 2 == 1:
+        for c in range(CHUNKS + 1):
+            if c < CHUNKS:
+                unit(1, c)
+            if c > 0:
+                subtract(c - 1)
+            if c < CHUNKS:
+                quantize_h(c)
+                second_stage(c)
+            if c > 0:
                 for i in range(2):
-                    scatter(i, (c - 1) * CH, (c + 1) * CH)
+                    scatter(i, (c - 1) * CH, c * CH)
+            if c > 0 and c + AHEAD < CHUNKS:
+                unit(0, c + AHEAD)
         for i in range(2, PACK):
             scatter(i, 0, S)

@@ -80,6 +80,15 @@ def tile_list_silhouette_atlas_features_kernel(
         load_wb(1, 0, room10[:])
         load_tab(1)
 
+        pages = {}
+
+        def clear_page(i, tag):
+            pages[i] = keep.tile([P, T2], F32, name=f"page{i}", tag=tag, align_bytes=64)
+            nc.vector.memset(pages[i][:].bitcast(I32), 0)
+
+        for i in range(3):
+            clear_page(i, f"page{i}")
+
         ts_got = keep.tile([P, S], U8, name="ts_got", tag="s2", align_bytes=64)
         nc.vector.tensor_copy(ts_got[:], ts_raw[:].indirect(pick[:]))
         staged = keep.tile([P, ROW], U8, name="staged", align_bytes=64)
@@ -228,7 +237,6 @@ def tile_list_silhouette_atlas_features_kernel(
                 diff[:, :, c * CH : (c + 1) * CH], banks_y[c][:], bd[q][:, :, col : col + CH], ALU.subtract
             )
 
-        pages = {}
         out_rows = out.rearrange("(p i) t -> p i t", i=PACK)
 
         def scatter(i, lo, hi):
@@ -249,12 +257,7 @@ def tile_list_silhouette_atlas_features_kernel(
         )
         gather_words(0, 1, "bf01")
         gather_words(1, 1, "w00")
-        pages[0] = keep.tile([P, T2], F32, name="page0", align_bytes=64)
-        nc.vector.memset(pages[0][:].bitcast(I32), 0)
-        for i, tag in ((1, "bf11"), (2, "tab0"), (3, "tab1")):
-            pages[i] = keep.tile([P, T2], F32, name=f"page{i}", tag=tag, align_bytes=64)
-            for lo in range(0, T2, 512):
-                nc.gpsimd.memset(pages[i][:, lo : lo + 512], 0.0)
+        clear_page(3, "s1")
         for c in range(CHUNKS + 1):
             if c < CHUNKS:
                 unit(1, c)
@@ -263,9 +266,12 @@ def tile_list_silhouette_atlas_features_kernel(
             if c < CHUNKS:
                 quantize_h(c)
                 second_stage(c)
-            if c > 0:
-                for i in range(2):
-                    scatter(i, (c - 1) * CH, c * CH)
+            if c % 2 == 1:
+                scatter(0, max(c - 2, 0) * CH, c * CH)
+            if c == CHUNKS:
+                scatter(0, (c - 1) * CH, c * CH)
+            if c > 0 and c % 2 == 0:
+                scatter(1, (c - 2) * CH, c * CH)
             if c > 0 and c + AHEAD < CHUNKS:
                 unit(0, c + AHEAD)
         for i in range(2, PACK):

@@ -24,7 +24,13 @@ BLOCKS = H // KP
 CH = 128
 CHUNKS = S // CH
 HALF = S // 2
+GROUP = 16
+QUAD = 32
+WS = H + N
+ROW = S + WS
+WB = PACK * KP
 AHEAD = 2
+RING = 4
 
 
 def tile_list_silhouette_atlas_features_kernel(
@@ -34,33 +40,31 @@ def tile_list_silhouette_atlas_features_kernel(
     with ExitStack() as ctx:
         lists = ctx.enter_context(tc.tile_pool(name="lists", bufs=1))
         keep = ctx.enter_context(tc.tile_pool(name="keep", bufs=1))
-        ring = ctx.enter_context(tc.tile_pool(name="ring", bufs=3))
+        ring = ctx.enter_context(tc.tile_pool(name="ring", bufs=RING))
         psum_ab = ctx.enter_context(tc.psum_pool(name="psum_ab", bufs=3))
         psum_y = ctx.enter_context(tc.psum_pool(name="psum_y", bufs=2))
 
-        pick = lists.tile([P, S // 16], U16, name="pick")
-        place = lists.tile([P, S // 16], U16, name="place")
+        pick = lists.tile([P, S // GROUP], U16, name="pick")
+        place = lists.tile([P, S // GROUP], U16, name="place")
 
-        WS = H + N
-        ROW = S + WS
-        ts_raw = keep.tile([P, T], U8, name="ts_raw", tag="s0", align_bytes=64)
-        ws_raw = keep.tile([P, WS], U8, name="ws_raw", tag="s1", align_bytes=64)
+        ts_raw = keep.tile([P, T], U8, name="ts_raw", tag="ts_raw", align_bytes=64)
+        ws_raw = keep.tile([P, WS], U8, name="ws_raw", tag="ws_raw", align_bytes=64)
         plane = keep.tile([P, PASSES * ROW], U8, name="plane", align_bytes=64)
         nc.vector.memset(ts_raw[:].bitcast(I32), 0)
         nc.vector.memset(ws_raw[:].bitcast(I32), 0)
-        warm_in = keep.tile([P, 1], F32, name="warm_in", tag="tab1", align_bytes=64)
-        warm_out = keep.tile([P, 1], F32, name="warm_out", tag="w00", align_bytes=64)
-        warm_bias = keep.tile([P, 1], F32, name="warm_bias", tag="w10", align_bytes=64)
-        nc.vector.memset(warm_in[:], 1.0)
-        nc.vector.memset(warm_bias[:], 1.0)
-        nc.scalar.activation(warm_out[:], warm_in[:], ACT.Abs_reciprocal_sqrt, bias=warm_bias[:])
+
+        one = keep.tile([P, 1], F32, name="one")
+        one_in = keep.tile([P, 1], F32, name="one_in", tag="tab1", align_bytes=64)
+        one_scale = keep.tile([P, 1], F32, name="one_scale", tag="wb_block0", align_bytes=64)
+        one_bias = keep.tile([P, 1], F32, name="one_bias", tag="wb01", align_bytes=64)
+        nc.vector.memset(one_in[:], 1.0)
+        nc.vector.memset(one_scale[:], 1.0)
+        nc.vector.memset(one_bias[:], 0.0)
+        nc.scalar.activation(one[:], one_in[:], ACT.Abs_reciprocal_sqrt, bias=one_bias[:], scale=one_scale[:])
         nc.vector.memset(plane[:].bitcast(I32), 0)
 
-        nc.sync.dma_start(pick[:], offs)
-        nc.sync.dma_start(place[:], offs2)
         tab = [keep.tile([P, T], I32, name=f"tab{a}", tag=f"tab{a}", align_bytes=64) for a in range(PASSES)]
         wb_raw = {}
-        WB = PACK * KP
 
         def load_tab(a):
             nc.sync.dma_start(tab[a][:], tab_words[a].rearrange("p t i -> p (t i)").bitcast(I32))
@@ -70,15 +74,18 @@ def tile_list_silhouette_atlas_features_kernel(
             rows = wb[a * KP : (a + 1) * KP, b * KP : (b + 1) * KP]
             nc.sync.dma_start(wb_raw[a, b], rows.rearrange("(p j) c -> p j c", j=PACK))
 
+        nc.sync.dma_start(pick[:], offs)
+        nc.sync.dma_start(place[:], offs2)
         load_tab(0)
         nc.sync.dma_start(ts_raw[0:P:4, :].bitcast(I32), tab_scales.bitcast(I32).rearrange("a q t -> q a t"))
         nc.sync.dma_start(ws_raw[0:P:4, 0:H].bitcast(I32), wa_scales.bitcast(I32).rearrange("a q c -> q a c"))
         nc.sync.dma_start(ws_raw[0:P:4, H:WS].bitcast(I32), wc_scales.bitcast(I32).rearrange("a q c -> q a c"))
-        room00 = keep.tile([P, WB], F32, name="room00", tag="w00", align_bytes=64)
-        room10 = keep.tile([P, WB], F32, name="room10", tag="w10", align_bytes=64)
-        load_wb(0, 0, room00[:])
-        load_wb(1, 0, room10[:])
+        wb_block0 = keep.tile([P, PASSES * WB], F32, name="wb_block0", tag="wb_block0", align_bytes=64)
+        for a in range(PASSES):
+            load_wb(a, 0, wb_block0[:, a * WB : (a + 1) * WB])
         load_tab(1)
+        wb01 = keep.tile([P, WB], F32, name="wb01", tag="wb01", align_bytes=64)
+        load_wb(0, 1, wb01[:])
 
         pages = {}
 
@@ -86,10 +93,10 @@ def tile_list_silhouette_atlas_features_kernel(
             pages[i] = keep.tile([P, T2], F32, name=f"page{i}", tag=tag, align_bytes=64)
             nc.vector.memset(pages[i][:].bitcast(I32), 0)
 
-        for i in range(3):
+        for i in range(PACK - 1):
             clear_page(i, f"page{i}")
 
-        ts_got = keep.tile([P, S], U8, name="ts_got", tag="s2", align_bytes=64)
+        ts_got = keep.tile([P, S], U8, name="ts_got", tag="ts_got", align_bytes=64)
         nc.vector.tensor_copy(ts_got[:], ts_raw[:].indirect(pick[:]))
         staged = keep.tile([P, ROW], U8, name="staged", align_bytes=64)
         nc.vector.tensor_copy(staged[:, 0:S].bitcast(I32), ts_got[:].bitcast(I32))
@@ -97,68 +104,69 @@ def tile_list_silhouette_atlas_features_kernel(
             staged[:, S:ROW].rearrange("p (g t m) -> p g t m", t=PACK, m=P),
             ws_raw[:].rearrange("p (g m t) -> p g t m", t=PACK, m=P),
         )
-        for d in range(4):
+        for d in range(P // QUAD):
             nc.sync.dma_start(
-                plane[32 * d : 32 * d + 4, :].bitcast(I32).rearrange("p (a c) -> p a c", a=PASSES),
-                staged[32 * d : 32 * d + 32 : 4, :].bitcast(I32),
+                plane[QUAD * d : QUAD * d + 4, :].bitcast(I32).rearrange("p (a c) -> p a c", a=PASSES),
+                staged[QUAD * d : QUAD * (d + 1) : 4, :].bitcast(I32),
             )
-        wa_raw = keep.tile([P, H], I32, name="wa_raw", tag="s1", align_bytes=64)
+        wa_raw = keep.tile([P, H], I32, name="wa_raw", tag="ts_got", align_bytes=64)
         nc.sync.dma_start(
             wa_raw[:].rearrange("p (a c) -> p a c", a=PASSES), wa_words.bitcast(I32).rearrange("a p c -> p a c")
         )
-        bd_rows = backdrop.rearrange("(p i) j -> p i j", i=PACK)
+        wb11 = keep.tile([P, WB], F32, name="wb11", tag="ws_raw", align_bytes=64)
+        load_wb(1, 1, wb11[:])
 
         got = {}
 
-        def gather_words(a, half, tag):
-            got[a, half] = keep.tile([P, HALF], U32, name=f"got{a}{half}", tag=tag, align_bytes=64)
-            cols = slice(half * HALF // 16, (half + 1) * HALF // 16)
-            nc.vector.tensor_copy(got[a, half][:], tab[a][:].bitcast(U32).indirect(pick[:, cols]))
+        def gather_words(a, lo, hi, tag):
+            words = keep.tile([P, hi - lo], U32, name=f"got{a}_{lo}", tag=tag, align_bytes=64)
+            nc.vector.tensor_copy(words[:], tab[a][:].bitcast(U32).indirect(pick[:, lo // GROUP : hi // GROUP]))
+            for c in range(lo // CH, hi // CH):
+                got[a, c] = words[:, c * CH - lo : (c + 1) * CH - lo]
 
         wb_codes, wb_scales = {}, {}
 
-        def quantize_wb(a, b, on_scalar):
-            rounded = keep.tile([P, KP * PACK], BF16, name=f"wb_bf{a}{b}", tag=f"bf{a}{b}", align_bytes=64)
-            dst = rounded[:].rearrange("p (t m j) -> p m t j", t=PACK, j=PACK)
-            src = wb_raw[a, b].rearrange("p j (m t) -> p m t j", t=PACK)
-            if on_scalar:
-                nc.scalar.copy(dst, src)
-            else:
-                nc.vector.tensor_copy(dst, src)
+        def quantize_wb(a, b, copy):
+            rounded = keep.tile([P, WB], BF16, name=f"wb_bf{a}{b}", tag=f"wb_bf{a}{b}", align_bytes=64)
+            copy(
+                rounded[:].rearrange("p (t m j) -> p m t j", t=PACK, j=PACK),
+                wb_raw[a, b].rearrange("p j (m t) -> p m t j", t=PACK),
+            )
             wb_codes[a, b] = keep.tile([P, KP], U32, name=f"wb_codes{a}{b}", align_bytes=64)
             wb_scales[a, b] = keep.tile([P, KP], U8, name=f"wb_scales{a}{b}", align_bytes=64)
             nc.vector.quantize_mx(out=wb_codes[a, b][:].bitcast(FP8X4), scales=wb_scales[a, b][:], in_=rounded[:])
 
-        gather_words(0, 0, "s0")
-        quantize_wb(0, 0, True)
-        wave3 = keep.tile([P, PASSES * WB], F32, name="wave3", tag="w00", align_bytes=64)
-        load_wb(0, 1, wave3[:, 0:WB])
-        load_wb(1, 1, wave3[:, WB : 2 * WB])
-        wc_raw = keep.tile([P, BLOCKS, N], I32, name="wc_raw", tag="bf00", align_bytes=64)
+        gather_words(0, 0, S, "ts_raw")
+        quantize_wb(0, 0, nc.scalar.copy)
+        wc_raw = keep.tile([P, BLOCKS, N], I32, name="wc_raw", tag="wb_bf00", align_bytes=64)
         nc.sync.dma_start(
-            wc_raw[:], wc_words.rearrange("a p c i -> a p (c i)").bitcast(I32).rearrange("a p c -> p a c")
+            wc_raw[:], wc_words.rearrange("b p c i -> b p (c i)").bitcast(I32).rearrange("b p c -> p b c")
         )
-        quantize_wb(1, 0, True)
-        gather_words(1, 0, "g10")
-        wave4 = keep.tile([P, (PACK + 1) * S], F32, name="wave4", tag="w10", align_bytes=64)
+        gather_words(1, 0, HALF, "got1_lo")
+        quantize_wb(1, 0, nc.scalar.copy)
+
+        tail_in = keep.tile([P, (PACK + 1) * S], F32, name="tail_in", tag="wb_bf10", align_bytes=64)
         bd = [
-            wave4[:, q * PACK * HALF : (q + 1) * PACK * HALF].rearrange("p (i j) -> p i j", i=PACK) for q in range(2)
+            tail_in[:, u * PACK * HALF : (u + 1) * PACK * HALF].rearrange("p (i j) -> p i j", i=PACK) for u in range(2)
         ]
-        weight = wave4[:, PACK * S : (PACK + 1) * S]
+        weight = tail_in[:, PACK * S : (PACK + 1) * S]
+        bd_rows = backdrop.rearrange("(p i) j -> p i j", i=PACK)
         nc.sync.dma_start(bd[0], bd_rows[:, :, 0:HALF])
         nc.sync.dma_start(weight, wgo)
         nc.sync.dma_start(bd[1], bd_rows[:, :, HALF:S])
+
+        gather_words(1, HALF, S, "got1_hi")
         wa_ord = keep.tile([P, PASSES * 2 * H], U8, name="wa_ord", align_bytes=64)
         nc.vector.tensor_copy(
-            wa_ord[:].bitcast(U16).rearrange("p (g t m) -> p g t m", g=PASSES * BLOCKS, t=PACK),
-            wa_raw[:].bitcast(U16).rearrange("p (g m t) -> p g t m", g=PASSES * BLOCKS, t=PACK),
+            wa_ord[:].bitcast(U16).rearrange("p (g t m) -> p g t m", t=PACK, m=P),
+            wa_raw[:].bitcast(U16).rearrange("p (g m t) -> p g t m", t=PACK, m=P),
         )
 
-        h_bf, h_codes, h_scales = {}, {}, {}
+        h_bf, h_codes, h_scales, banks_y = {}, {}, {}, {}
         diff = keep.tile([P, PACK, S], F32, name="diff")
+        wc_ord = keep.tile([P, BLOCKS * N], U32, name="wc_ord", align_bytes=64)
 
         def unit(b, c):
-            half, col = divmod(c * CH, HALF)
             bank_a = psum_ab.tile([P, PACK, CH], F32, name="bank_a")
             bank_b = psum_ab.tile([P, PACK, CH], F32, name="bank_b")
             for t in range(PACK):
@@ -167,30 +175,30 @@ def tile_list_silhouette_atlas_features_kernel(
                         out=bank_b[:, t, :],
                         lhsT=wb_codes[a, b][:, t * P : (t + 1) * P].bitcast(FP8X4),
                         lhsT_scale=wb_scales[a, b][:, t * P : (t + 1) * P],
-                        rhs=got[a, half][:, col : col + CH].bitcast(FP8X4),
+                        rhs=got[a, c].bitcast(FP8X4),
                         rhs_scale=plane[:, a * ROW + c * CH : a * ROW + (c + 1) * CH],
                         start=(a == 0),
                         stop=(a == PASSES - 1),
                     )
             for t in range(PACK):
                 for a in range(PASSES):
-                    w0 = a * H + b * KP + t * P
-                    s0 = a * ROW + S + b * KP + t * P
+                    word0 = a * H + b * KP + t * P
+                    scale0 = a * ROW + S + b * KP + t * P
                     nc.tensor.matmul_mx(
                         out=bank_a[:, t, :],
-                        lhsT=wa_ord[:, 2 * w0 : 2 * (w0 + P)].bitcast(FP4X4),
-                        lhsT_scale=plane[:, s0 : s0 + P],
-                        rhs=got[a, half][:, col : col + CH].bitcast(FP8X4),
+                        lhsT=wa_ord[:, 2 * word0 : 2 * (word0 + P)].bitcast(FP4X4),
+                        lhsT_scale=plane[:, scale0 : scale0 + P],
+                        rhs=got[a, c].bitcast(FP8X4),
                         rhs_scale=plane[:, a * ROW + c * CH : a * ROW + (c + 1) * CH],
                         start=(a == 0),
                         stop=(a == PASSES - 1),
                     )
-            size = ring.tile([P, CH * PACK], F32, name="size")
-            root = ring.tile([P, CH * PACK], F32, name="root")
+            size = ring.tile([P, KP], F32, name="size")
+            root = ring.tile([P, KP], F32, name="root")
             nc.scalar.activation(
-                size[:].rearrange("p (n t) -> p n t", t=PACK), bank_b[:].rearrange("p t n -> p n t"), ACT.Abs
+                size[:].rearrange("p (j t) -> p j t", t=PACK), bank_b[:].rearrange("p t j -> p j t"), ACT.Abs
             )
-            nc.scalar.activation(root[:], size[:], ACT.Abs_reciprocal_sqrt, bias=1.0)
+            nc.scalar.activation(root[:], size[:], ACT.Abs_reciprocal_sqrt, bias=one[:])
             if b == 1 and c > 0:
                 recip = diff[:, :, (c - 1) * CH : c * CH]
             else:
@@ -200,71 +208,61 @@ def tile_list_silhouette_atlas_features_kernel(
             if b == 0:
                 h_bf[c] = keep.tile([P, BLOCKS * KP], BF16, name=f"h_bf{c}", align_bytes=64)
             nc.vector.tensor_tensor(
-                h_bf[c][:, b * KP : (b + 1) * KP].rearrange("p (g n t) -> p g n t", g=PACK, t=PACK),
-                bank_a[:].rearrange("p t (g n) -> p g n t", g=PACK),
-                recip.rearrange("p g (n t) -> p g n t", t=PACK),
+                h_bf[c][:, b * KP : (b + 1) * KP].rearrange("p (g j t) -> p g j t", g=PACK, t=PACK),
+                bank_a[:].rearrange("p t (g j) -> p g j t", g=PACK),
+                recip.rearrange("p g (j t) -> p g j t", t=PACK),
                 ALU.mult,
             )
 
-        def quantize_h(c):
+        def second_stage(c):
             h_codes[c] = keep.tile([P, BLOCKS * CH], U32, name=f"h_codes{c}", align_bytes=64)
             h_scales[c] = keep.tile([P, BLOCKS * CH], U8, name=f"h_scales{c}", align_bytes=64)
             nc.vector.quantize_mx(out=h_codes[c][:].bitcast(FP8X4), scales=h_scales[c][:], in_=h_bf[c][:])
-
-        wc_ord = keep.tile([P, BLOCKS * N], U32, name="wc_ord", align_bytes=64)
-
-        banks_y = {}
-
-        def second_stage(c):
-            bank_y = psum_y.tile([P, PACK, CH], F32, name="bank_y")
+            banks_y[c] = psum_y.tile([P, PACK, CH], F32, name="bank_y")
             for i in range(PACK):
                 for b in range(BLOCKS):
-                    s0 = b * ROW + S + H + i * P
+                    scale0 = b * ROW + S + H + i * P
                     nc.tensor.matmul_mx(
-                        out=bank_y[:, i, :],
+                        out=banks_y[c][:, i, :],
                         lhsT=wc_ord[:, b * N + i * P : b * N + (i + 1) * P].bitcast(FP8X4),
-                        lhsT_scale=plane[:, s0 : s0 + P],
+                        lhsT_scale=plane[:, scale0 : scale0 + P],
                         rhs=h_codes[c][:, b * CH : (b + 1) * CH].bitcast(FP8X4),
                         rhs_scale=h_scales[c][:, b * CH : (b + 1) * CH],
                         start=(b == 0),
                         stop=(b == BLOCKS - 1),
                     )
-            banks_y[c] = bank_y
 
         def subtract(c):
-            q, col = divmod(c * CH, HALF)
+            u, col = divmod(c * CH, HALF)
             nc.vector.tensor_tensor(
-                diff[:, :, c * CH : (c + 1) * CH], banks_y[c][:], bd[q][:, :, col : col + CH], ALU.subtract
+                diff[:, :, c * CH : (c + 1) * CH], banks_y[c][:], bd[u][:, :, col : col + CH], ALU.subtract
             )
 
         out_rows = out.rearrange("(p i) t -> p i t", i=PACK)
 
         def scatter(i, lo, hi):
             nc.vector.tensor_tensor(
-                pages[i][:].indirect(place[:, lo // 16 : hi // 16]), diff[:, i, lo:hi], weight[:, lo:hi], ALU.mult
+                pages[i][:].indirect(place[:, lo // GROUP : hi // GROUP]), diff[:, i, lo:hi], weight[:, lo:hi], ALU.mult
             )
             if hi == S:
                 nc.sync.dma_start(out_rows[:, i, :], pages[i][:])
 
-        unit(0, 0)
-        unit(0, 1)
-        quantize_wb(0, 1, False)
-        quantize_wb(1, 1, False)
-        unit(0, 2)
+        for c in range(AHEAD):
+            unit(0, c)
+        for a in range(PASSES):
+            quantize_wb(a, 1, nc.vector.tensor_copy)
+        unit(0, AHEAD)
+        clear_page(PACK - 1, "wb_block0")
         nc.vector.tensor_copy(
             wc_ord[:].bitcast(I32).rearrange("p (b i g m) -> p b g i m", b=BLOCKS, i=PACK, m=4),
             wc_raw[:].rearrange("p b (g m i) -> p b g i m", i=PACK, m=4),
         )
-        gather_words(0, 1, "bf01")
-        gather_words(1, 1, "w00")
-        clear_page(3, "s1")
         for c in range(CHUNKS + 1):
             if c < CHUNKS:
                 unit(1, c)
             if c > 0:
                 subtract(c - 1)
             if c < CHUNKS:
-                quantize_h(c)
                 second_stage(c)
             if c % 2 == 1:
                 scatter(0, max(c - 2, 0) * CH, c * CH)

@@ -29,7 +29,8 @@ QUAD = 32
 WS = H + N
 ROW = S + WS
 WB = PACK * KP
-AHEAD = 2
+AHEAD = 3
+FIRST = 2 * CH
 RING = 4
 
 
@@ -54,9 +55,9 @@ def tile_list_silhouette_atlas_features_kernel(
         nc.vector.memset(ws_raw[:].bitcast(I32), 0)
 
         one = keep.tile([P, 1], F32, name="one")
-        one_in = keep.tile([P, 1], F32, name="one_in", tag="tab1", align_bytes=64)
-        one_scale = keep.tile([P, 1], F32, name="one_scale", tag="wb_block0", align_bytes=64)
-        one_bias = keep.tile([P, 1], F32, name="one_bias", tag="wb01", align_bytes=64)
+        one_in = keep.tile([P, 1], F32, name="one_in", tag="tab0", align_bytes=64)
+        one_scale = keep.tile([P, 1], F32, name="one_scale", tag="wb_pair", align_bytes=64)
+        one_bias = keep.tile([P, 1], F32, name="one_bias", tag="tab1", align_bytes=64)
         nc.vector.memset(one_in[:], 1.0)
         nc.vector.memset(one_scale[:], 1.0)
         nc.vector.memset(one_bias[:], 0.0)
@@ -76,36 +77,27 @@ def tile_list_silhouette_atlas_features_kernel(
 
         nc.sync.dma_start(pick[:], offs)
         nc.sync.dma_start(place[:], offs2)
-        load_tab(0)
+        wb00 = keep.tile([P, WB], F32, name="wb00", align_bytes=64)
+        load_wb(0, 0, wb00[:])
         nc.sync.dma_start(ts_raw[0:P:4, :].bitcast(I32), tab_scales.bitcast(I32).rearrange("a q t -> q a t"))
         nc.sync.dma_start(ws_raw[0:P:4, 0:H].bitcast(I32), wa_scales.bitcast(I32).rearrange("a q c -> q a c"))
         nc.sync.dma_start(ws_raw[0:P:4, H:WS].bitcast(I32), wc_scales.bitcast(I32).rearrange("a q c -> q a c"))
-        wb_block0 = keep.tile([P, PASSES * WB], F32, name="wb_block0", tag="wb_block0", align_bytes=64)
+        wb_pair = keep.tile([P, 2 * WB], F32, name="wb_pair", tag="wb_pair", align_bytes=64)
+        load_wb(1, 0, wb_pair[:, 0:WB])
+        load_wb(0, 1, wb_pair[:, WB : 2 * WB])
         for a in range(PASSES):
-            load_wb(a, 0, wb_block0[:, a * WB : (a + 1) * WB])
-        load_tab(1)
-        wb01 = keep.tile([P, WB], F32, name="wb01", tag="wb01", align_bytes=64)
-        load_wb(0, 1, wb01[:])
-
-        pages = {}
-
-        def clear_page(i, tag):
-            pages[i] = keep.tile([P, T2], F32, name=f"page{i}", tag=tag, align_bytes=64)
-            nc.vector.memset(pages[i][:].bitcast(I32), 0)
-
-        for i in range(PACK - 1):
-            clear_page(i, f"page{i}")
+            load_tab(a)
 
         ts_got = keep.tile([P, S], U8, name="ts_got", tag="ts_got", align_bytes=64)
         nc.vector.tensor_copy(ts_got[:], ts_raw[:].indirect(pick[:]))
-        staged = keep.tile([P, ROW], U8, name="staged", align_bytes=64)
+        staged = keep.tile([P, ROW], U8, name="staged", tag="staged", align_bytes=64)
         nc.vector.tensor_copy(staged[:, 0:S].bitcast(I32), ts_got[:].bitcast(I32))
         nc.vector.tensor_copy(
             staged[:, S:ROW].rearrange("p (g t m) -> p g t m", t=PACK, m=P),
             ws_raw[:].rearrange("p (g m t) -> p g t m", t=PACK, m=P),
         )
         for d in range(P // QUAD):
-            nc.sync.dma_start(
+            nc.scalar.dma_start(
                 plane[QUAD * d : QUAD * d + 4, :].bitcast(I32).rearrange("p (a c) -> p a c", a=PASSES),
                 staged[QUAD * d : QUAD * (d + 1) : 4, :].bitcast(I32),
             )
@@ -136,16 +128,16 @@ def tile_list_silhouette_atlas_features_kernel(
             wb_scales[a, b] = keep.tile([P, KP], U8, name=f"wb_scales{a}{b}", align_bytes=64)
             nc.vector.quantize_mx(out=wb_codes[a, b][:].bitcast(FP8X4), scales=wb_scales[a, b][:], in_=rounded[:])
 
-        gather_words(0, 0, S, "ts_raw")
         quantize_wb(0, 0, nc.scalar.copy)
-        wc_raw = keep.tile([P, BLOCKS, N], I32, name="wc_raw", tag="wb_bf00", align_bytes=64)
+        quantize_wb(1, 0, nc.scalar.copy)
+        gather_words(0, 0, S, "ts_raw")
+        quantize_wb(0, 1, nc.scalar.copy)
+        wc_raw = keep.tile([P, BLOCKS, N], I32, name="wc_raw", tag="staged", align_bytes=64)
         nc.sync.dma_start(
             wc_raw[:], wc_words.rearrange("b p c i -> b p (c i)").bitcast(I32).rearrange("b p c -> p b c")
         )
-        gather_words(1, 0, HALF, "got1_lo")
-        quantize_wb(1, 0, nc.scalar.copy)
 
-        tail_in = keep.tile([P, (PACK + 1) * S], F32, name="tail_in", tag="wb_bf10", align_bytes=64)
+        tail_in = keep.tile([P, (PACK + 1) * S], F32, name="tail_in", tag="wb_bf01", align_bytes=64)
         bd = [
             tail_in[:, u * PACK * HALF : (u + 1) * PACK * HALF].rearrange("p (i j) -> p i j", i=PACK) for u in range(2)
         ]
@@ -155,12 +147,13 @@ def tile_list_silhouette_atlas_features_kernel(
         nc.sync.dma_start(weight, wgo)
         nc.sync.dma_start(bd[1], bd_rows[:, :, HALF:S])
 
-        gather_words(1, HALF, S, "got1_hi")
-        wa_ord = keep.tile([P, PASSES * 2 * H], U8, name="wa_ord", align_bytes=64)
-        nc.vector.tensor_copy(
-            wa_ord[:].bitcast(U16).rearrange("p (g t m) -> p g t m", t=PACK, m=P),
-            wa_raw[:].bitcast(U16).rearrange("p (g m t) -> p g t m", t=PACK, m=P),
-        )
+        wa_ord = [keep.tile([P, PASSES * 2 * KP], U8, name=f"wa_ord{b}", align_bytes=64) for b in range(BLOCKS)]
+
+        def order_wa(b):
+            nc.vector.tensor_copy(
+                wa_ord[b][:].bitcast(U16).rearrange("p (a t m) -> p a t m", t=PACK, m=P),
+                wa_raw[:].bitcast(U16).rearrange("p (a b m t) -> p b a t m", b=BLOCKS, t=PACK, m=P)[:, b],
+            )
 
         h_bf, h_codes, h_scales, banks_y = {}, {}, {}, {}
         diff = keep.tile([P, PACK, S], F32, name="diff")
@@ -182,11 +175,11 @@ def tile_list_silhouette_atlas_features_kernel(
                     )
             for t in range(PACK):
                 for a in range(PASSES):
-                    word0 = a * H + b * KP + t * P
+                    word0 = a * KP + t * P
                     scale0 = a * ROW + S + b * KP + t * P
                     nc.tensor.matmul_mx(
                         out=bank_a[:, t, :],
-                        lhsT=wa_ord[:, 2 * word0 : 2 * (word0 + P)].bitcast(FP4X4),
+                        lhsT=wa_ord[b][:, 2 * word0 : 2 * (word0 + P)].bitcast(FP4X4),
                         lhsT_scale=plane[:, scale0 : scale0 + P],
                         rhs=got[a, c].bitcast(FP8X4),
                         rhs_scale=plane[:, a * ROW + c * CH : a * ROW + (c + 1) * CH],
@@ -194,23 +187,25 @@ def tile_list_silhouette_atlas_features_kernel(
                         stop=(a == PASSES - 1),
                     )
             size = ring.tile([P, KP], F32, name="size")
-            root = ring.tile([P, KP], F32, name="root")
             nc.scalar.activation(
                 size[:].rearrange("p (j t) -> p j t", t=PACK), bank_b[:].rearrange("p t j -> p j t"), ACT.Abs
             )
-            nc.scalar.activation(root[:], size[:], ACT.Abs_reciprocal_sqrt, bias=one[:])
             if b == 1 and c > 0:
-                recip = diff[:, :, (c - 1) * CH : c * CH]
+                root = diff[:, :, (c - 1) * CH : c * CH]
             else:
                 spare = ring.tile([P, PACK, CH], F32, name="spare")
-                recip = spare[:]
-            nc.scalar.activation(recip, root[:].rearrange("p (g x) -> p g x", g=PACK), ACT.Square)
+                root = spare[:]
+            nc.scalar.activation(
+                root, size[:].rearrange("p (g x) -> p g x", g=PACK), ACT.Abs_reciprocal_sqrt, bias=one[:]
+            )
+            recip = ring.tile([P, KP], F32, name="recip")
+            nc.scalar.activation(recip[:].rearrange("p (g x) -> p g x", g=PACK), root, ACT.Square)
             if b == 0:
                 h_bf[c] = keep.tile([P, BLOCKS * KP], BF16, name=f"h_bf{c}", align_bytes=64)
             nc.vector.tensor_tensor(
-                h_bf[c][:, b * KP : (b + 1) * KP].rearrange("p (g j t) -> p g j t", g=PACK, t=PACK),
-                bank_a[:].rearrange("p t (g j) -> p g j t", g=PACK),
-                recip.rearrange("p g (j t) -> p g j t", t=PACK),
+                h_bf[c][:, b * KP : (b + 1) * KP].rearrange("p (j t) -> p j t", t=PACK),
+                bank_a[:].rearrange("p t j -> p j t"),
+                recip[:].rearrange("p (j t) -> p j t", t=PACK),
                 ALU.mult,
             )
 
@@ -240,37 +235,41 @@ def tile_list_silhouette_atlas_features_kernel(
 
         out_rows = out.rearrange("(p i) t -> p i t", i=PACK)
 
-        def scatter(i, lo, hi):
+        pages = [keep.tile([P, T2], F32, name=f"page{i}", align_bytes=64) for i in range(PACK)]
+        placed = [0] * PACK
+
+        def scatter(i, hi):
+            lo = placed[i]
             nc.vector.tensor_tensor(
                 pages[i][:].indirect(place[:, lo // GROUP : hi // GROUP]), diff[:, i, lo:hi], weight[:, lo:hi], ALU.mult
             )
+            placed[i] = hi
             if hi == S:
                 nc.sync.dma_start(out_rows[:, i, :], pages[i][:])
 
+        gather_words(1, 0, FIRST, "got1_lo")
+        order_wa(0)
+        gather_words(1, FIRST, S, "got1_hi")
+        quantize_wb(1, 1, nc.vector.tensor_copy)
         for c in range(AHEAD):
             unit(0, c)
-        for a in range(PASSES):
-            quantize_wb(a, 1, nc.vector.tensor_copy)
-        unit(0, AHEAD)
-        clear_page(PACK - 1, "wb_block0")
+        order_wa(1)
         nc.vector.tensor_copy(
             wc_ord[:].bitcast(I32).rearrange("p (b i g m) -> p b g i m", b=BLOCKS, i=PACK, m=4),
             wc_raw[:].rearrange("p b (g m i) -> p b g i m", i=PACK, m=4),
         )
-        for c in range(CHUNKS + 1):
-            if c < CHUNKS:
-                unit(1, c)
+        for page in pages:
+            for u in range(2):
+                nc.vector.memset(page[:, u * T2 // 2 : (u + 1) * T2 // 2].bitcast(I32), 0)
+        for c in range(CHUNKS):
+            if c >= AHEAD:
+                unit(0, c)
+            unit(1, c)
             if c > 0:
                 subtract(c - 1)
-            if c < CHUNKS:
-                second_stage(c)
-            if c % 2 == 1:
-                scatter(0, max(c - 2, 0) * CH, c * CH)
-            if c == CHUNKS:
-                scatter(0, (c - 1) * CH, c * CH)
-            if c > 0 and c % 2 == 0:
-                scatter(1, (c - 2) * CH, c * CH)
-            if c > 0 and c + AHEAD < CHUNKS:
-                unit(0, c + AHEAD)
-        for i in range(2, PACK):
-            scatter(i, 0, S)
+            second_stage(c)
+            if c > 0:
+                scatter((c - 1) % PACK, c * CH)
+        subtract(CHUNKS - 1)
+        for i in sorted(range(PACK), key=lambda page: S - placed[page]):
+            scatter(i, S)

@@ -23,13 +23,11 @@ PASSES = K // KP
 BLOCKS = H // KP
 CH = 128
 CHUNKS = S // CH
-HALF = S // 2
+EARLY = 2 * CH
 GROUP = 16
 QUAD = 32
 WS = H + N
-ROW = S + WS
 WB = PACK * KP
-AHEAD = 3
 FIRST = 2 * CH
 RING = 4
 
@@ -50,63 +48,60 @@ def tile_list_silhouette_atlas_features_kernel(
 
         ts_raw = keep.tile([P, T], U8, name="ts_raw", tag="ts_raw", align_bytes=64)
         ws_raw = keep.tile([P, WS], U8, name="ws_raw", tag="ws_raw", align_bytes=64)
-        plane = keep.tile([P, PASSES * ROW], U8, name="plane", align_bytes=64)
+        plane_v = keep.tile([P, PASSES * S], U8, name="plane_v", align_bytes=64)
         nc.vector.memset(ts_raw[:].bitcast(I32), 0)
         nc.vector.memset(ws_raw[:].bitcast(I32), 0)
 
         one = keep.tile([P, 1], F32, name="one")
-        one_in = keep.tile([P, 1], F32, name="one_in", tag="tab0", align_bytes=64)
-        one_scale = keep.tile([P, 1], F32, name="one_scale", tag="wb_pair", align_bytes=64)
-        one_bias = keep.tile([P, 1], F32, name="one_bias", tag="tab1", align_bytes=64)
+        one_in = keep.tile([P, 1], F32, name="one_in", tag="wb10", align_bytes=64)
+        one_scale = keep.tile([P, 1], F32, name="one_scale", tag="wb01", align_bytes=64)
+        one_bias = keep.tile([P, 1], F32, name="one_bias", tag="tab0", align_bytes=64)
         nc.vector.memset(one_in[:], 1.0)
         nc.vector.memset(one_scale[:], 1.0)
         nc.vector.memset(one_bias[:], 0.0)
         nc.scalar.activation(one[:], one_in[:], ACT.Abs_reciprocal_sqrt, bias=one_bias[:], scale=one_scale[:])
-        nc.vector.memset(plane[:].bitcast(I32), 0)
+        nc.vector.memset(plane_v[:].bitcast(I32), 0)
 
-        tab = [keep.tile([P, T], I32, name=f"tab{a}", tag=f"tab{a}", align_bytes=64) for a in range(PASSES)]
+        tab = {}
         wb_raw = {}
 
-        def load_tab(a):
+        def load_tab(a, tag):
+            tab[a] = keep.tile([P, T], I32, name=f"tab{a}", tag=tag, align_bytes=64)
             nc.sync.dma_start(tab[a][:], tab_words[a].rearrange("p t i -> p (t i)").bitcast(I32))
 
-        def load_wb(a, b, room):
-            wb_raw[a, b] = room.rearrange("p (j c) -> p j c", j=PACK)
+        def load_wb(a, b, tag):
+            room = keep.tile([P, WB], F32, name=f"wb{a}{b}", tag=tag, align_bytes=64)
+            wb_raw[a, b] = room[:].rearrange("p (j c) -> p j c", j=PACK)
             rows = wb[a * KP : (a + 1) * KP, b * KP : (b + 1) * KP]
             nc.sync.dma_start(wb_raw[a, b], rows.rearrange("(p j) c -> p j c", j=PACK))
 
         nc.sync.dma_start(pick[:], offs)
         nc.sync.dma_start(place[:], offs2)
-        wb00 = keep.tile([P, WB], F32, name="wb00", align_bytes=64)
-        load_wb(0, 0, wb00[:])
-        nc.sync.dma_start(ts_raw[0:P:4, :].bitcast(I32), tab_scales.bitcast(I32).rearrange("a q t -> q a t"))
-        nc.sync.dma_start(ws_raw[0:P:4, 0:H].bitcast(I32), wa_scales.bitcast(I32).rearrange("a q c -> q a c"))
-        nc.sync.dma_start(ws_raw[0:P:4, H:WS].bitcast(I32), wc_scales.bitcast(I32).rearrange("a q c -> q a c"))
-        wb_pair = keep.tile([P, 2 * WB], F32, name="wb_pair", tag="wb_pair", align_bytes=64)
-        load_wb(1, 0, wb_pair[:, 0:WB])
-        load_wb(0, 1, wb_pair[:, WB : 2 * WB])
-        for a in range(PASSES):
-            load_tab(a)
+        load_wb(0, 0, "wb00")
+        nc.scalar.dma_start(ts_raw[0:P:4, :].bitcast(I32), tab_scales.bitcast(I32).rearrange("a q t -> q a t"))
+        nc.scalar.dma_start(ws_raw[0:P:4, 0:H].bitcast(I32), wa_scales.bitcast(I32).rearrange("a q c -> q a c"))
+        nc.scalar.dma_start(ws_raw[0:P:4, H:WS].bitcast(I32), wc_scales.bitcast(I32).rearrange("a q c -> q a c"))
+        load_wb(1, 0, "wb10")
+        load_wb(0, 1, "wb01")
+        load_tab(0, "tab0")
+
+        def move_rows(plane, rows):
+            for d in range(P // QUAD):
+                nc.sync.dma_start(
+                    plane[QUAD * d : QUAD * d + 4, :].bitcast(I32).rearrange("p (a c) -> p a c", a=PASSES),
+                    rows[QUAD * d : QUAD * (d + 1) : 4, :].bitcast(I32),
+                )
 
         ts_got = keep.tile([P, S], U8, name="ts_got", tag="ts_got", align_bytes=64)
         nc.vector.tensor_copy(ts_got[:], ts_raw[:].indirect(pick[:]))
-        staged = keep.tile([P, ROW], U8, name="staged", tag="staged", align_bytes=64)
-        nc.vector.tensor_copy(staged[:, 0:S].bitcast(I32), ts_got[:].bitcast(I32))
+        move_rows(plane_v, ts_got)
+        load_tab(1, "ts_raw")
+        ws_ord = keep.tile([P, WS], U8, name="ws_ord", align_bytes=64)
         nc.vector.tensor_copy(
-            staged[:, S:ROW].rearrange("p (g t m) -> p g t m", t=PACK, m=P),
+            ws_ord[:].rearrange("p (g t m) -> p g t m", t=PACK, m=P),
             ws_raw[:].rearrange("p (g m t) -> p g t m", t=PACK, m=P),
         )
-        for d in range(P // QUAD):
-            nc.scalar.dma_start(
-                plane[QUAD * d : QUAD * d + 4, :].bitcast(I32).rearrange("p (a c) -> p a c", a=PASSES),
-                staged[QUAD * d : QUAD * (d + 1) : 4, :].bitcast(I32),
-            )
-        wa_raw = keep.tile([P, H], I32, name="wa_raw", tag="ts_got", align_bytes=64)
-        nc.sync.dma_start(
-            wa_raw[:].rearrange("p (a c) -> p a c", a=PASSES), wa_words.bitcast(I32).rearrange("a p c -> p a c")
-        )
-        wb11 = keep.tile([P, WB], F32, name="wb11", tag="ws_raw", align_bytes=64)
-        load_wb(1, 1, wb11[:])
+        load_wb(1, 1, "ws_raw")
 
         got = {}
 
@@ -118,34 +113,28 @@ def tile_list_silhouette_atlas_features_kernel(
 
         wb_codes, wb_scales = {}, {}
 
-        def quantize_wb(a, b, copy):
+        def quantize_wb(a, b, copy, tag):
             rounded = keep.tile([P, WB], BF16, name=f"wb_bf{a}{b}", tag=f"wb_bf{a}{b}", align_bytes=64)
             copy(
                 rounded[:].rearrange("p (t m j) -> p m t j", t=PACK, j=PACK),
                 wb_raw[a, b].rearrange("p j (m t) -> p m t j", t=PACK),
             )
-            wb_codes[a, b] = keep.tile([P, KP], U32, name=f"wb_codes{a}{b}", align_bytes=64)
+            wb_codes[a, b] = keep.tile([P, KP], U32, name=f"wb_codes{a}{b}", tag=tag, align_bytes=64)
             wb_scales[a, b] = keep.tile([P, KP], U8, name=f"wb_scales{a}{b}", align_bytes=64)
             nc.vector.quantize_mx(out=wb_codes[a, b][:].bitcast(FP8X4), scales=wb_scales[a, b][:], in_=rounded[:])
 
-        quantize_wb(0, 0, nc.scalar.copy)
-        quantize_wb(1, 0, nc.scalar.copy)
-        gather_words(0, 0, S, "ts_raw")
-        quantize_wb(0, 1, nc.scalar.copy)
-        wc_raw = keep.tile([P, BLOCKS, N], I32, name="wc_raw", tag="staged", align_bytes=64)
+        quantize_wb(0, 0, nc.scalar.copy, "codes00")
+        quantize_wb(1, 0, nc.scalar.copy, "codes10")
+        plane_w = keep.tile([P, PASSES * WS], U8, name="plane_w", tag="wb_bf10", align_bytes=64)
+        nc.vector.memset(plane_w[:].bitcast(I32), 0)
+        move_rows(plane_w, ws_ord)
+        gather_words(0, 0, S, "got0")
+        gather_words(1, 0, FIRST, "got1_lo")
+        quantize_wb(0, 1, nc.scalar.copy, "tab0")
+        wa_raw = keep.tile([P, H], I32, name="wa_raw", tag="wb01", align_bytes=64)
         nc.sync.dma_start(
-            wc_raw[:], wc_words.rearrange("b p c i -> b p (c i)").bitcast(I32).rearrange("b p c -> p b c")
+            wa_raw[:].rearrange("p (a c) -> p a c", a=PASSES), wa_words.bitcast(I32).rearrange("a p c -> p a c")
         )
-
-        tail_in = keep.tile([P, (PACK + 1) * S], F32, name="tail_in", tag="wb_bf01", align_bytes=64)
-        bd = [
-            tail_in[:, u * PACK * HALF : (u + 1) * PACK * HALF].rearrange("p (i j) -> p i j", i=PACK) for u in range(2)
-        ]
-        weight = tail_in[:, PACK * S : (PACK + 1) * S]
-        bd_rows = backdrop.rearrange("(p i) j -> p i j", i=PACK)
-        nc.sync.dma_start(bd[0], bd_rows[:, :, 0:HALF])
-        nc.sync.dma_start(weight, wgo)
-        nc.sync.dma_start(bd[1], bd_rows[:, :, HALF:S])
 
         wa_ord = [keep.tile([P, PASSES * 2 * KP], U8, name=f"wa_ord{b}", align_bytes=64) for b in range(BLOCKS)]
 
@@ -159,8 +148,7 @@ def tile_list_silhouette_atlas_features_kernel(
         diff = keep.tile([P, PACK, S], F32, name="diff")
         wc_ord = keep.tile([P, BLOCKS * N], U32, name="wc_ord", align_bytes=64)
 
-        def unit(b, c):
-            bank_a = psum_ab.tile([P, PACK, CH], F32, name="bank_a")
+        def product_b(b, c):
             bank_b = psum_ab.tile([P, PACK, CH], F32, name="bank_b")
             for t in range(PACK):
                 for a in range(PASSES):
@@ -169,45 +157,60 @@ def tile_list_silhouette_atlas_features_kernel(
                         lhsT=wb_codes[a, b][:, t * P : (t + 1) * P].bitcast(FP8X4),
                         lhsT_scale=wb_scales[a, b][:, t * P : (t + 1) * P],
                         rhs=got[a, c].bitcast(FP8X4),
-                        rhs_scale=plane[:, a * ROW + c * CH : a * ROW + (c + 1) * CH],
+                        rhs_scale=plane_v[:, a * S + c * CH : a * S + (c + 1) * CH],
                         start=(a == 0),
                         stop=(a == PASSES - 1),
                     )
+            return bank_b
+
+        def product_a(b, c):
+            bank_a = psum_ab.tile([P, PACK, CH], F32, name="bank_a")
             for t in range(PACK):
                 for a in range(PASSES):
                     word0 = a * KP + t * P
-                    scale0 = a * ROW + S + b * KP + t * P
+                    scale0 = a * WS + b * KP + t * P
                     nc.tensor.matmul_mx(
                         out=bank_a[:, t, :],
                         lhsT=wa_ord[b][:, 2 * word0 : 2 * (word0 + P)].bitcast(FP4X4),
-                        lhsT_scale=plane[:, scale0 : scale0 + P],
+                        lhsT_scale=plane_w[:, scale0 : scale0 + P],
                         rhs=got[a, c].bitcast(FP8X4),
-                        rhs_scale=plane[:, a * ROW + c * CH : a * ROW + (c + 1) * CH],
+                        rhs_scale=plane_v[:, a * S + c * CH : a * S + (c + 1) * CH],
                         start=(a == 0),
                         stop=(a == PASSES - 1),
                     )
-            size = ring.tile([P, KP], F32, name="size")
-            nc.scalar.activation(
-                size[:].rearrange("p (j t) -> p j t", t=PACK), bank_b[:].rearrange("p t j -> p j t"), ACT.Abs
-            )
-            if b == 1 and c > 0:
-                root = diff[:, :, (c - 1) * CH : c * CH]
-            else:
-                spare = ring.tile([P, PACK, CH], F32, name="spare")
-                root = spare[:]
-            nc.scalar.activation(
-                root, size[:].rearrange("p (g x) -> p g x", g=PACK), ACT.Abs_reciprocal_sqrt, bias=one[:]
-            )
-            recip = ring.tile([P, KP], F32, name="recip")
-            nc.scalar.activation(recip[:].rearrange("p (g x) -> p g x", g=PACK), root, ACT.Square)
-            if b == 0:
-                h_bf[c] = keep.tile([P, BLOCKS * KP], BF16, name=f"h_bf{c}", align_bytes=64)
-            nc.vector.tensor_tensor(
-                h_bf[c][:, b * KP : (b + 1) * KP].rearrange("p (j t) -> p j t", t=PACK),
-                bank_a[:].rearrange("p t j -> p j t"),
-                recip[:].rearrange("p (j t) -> p j t", t=PACK),
-                ALU.mult,
-            )
+            return bank_a
+
+        def unit_pair(units):
+            banks_b = [product_b(b, c) for b, c in units]
+            banks_a = [product_a(b, c) for b, c in units]
+            sizes, roots = [], []
+            for bank_b in banks_b:
+                size = ring.tile([P, KP], F32, name="size")
+                nc.scalar.activation(
+                    size[:].rearrange("p (j t) -> p j t", t=PACK), bank_b[:].rearrange("p t j -> p j t"), ACT.Abs
+                )
+                sizes.append(size)
+            for (b, c), size in zip(units, sizes):
+                if b == 1 and c > 0:
+                    root = diff[:, :, (c - 1) * CH : c * CH]
+                else:
+                    spare = ring.tile([P, PACK, CH], F32, name="spare")
+                    root = spare[:]
+                nc.scalar.activation(
+                    root, size[:].rearrange("p (g x) -> p g x", g=PACK), ACT.Abs_reciprocal_sqrt, bias=one[:]
+                )
+                roots.append(root)
+            for (b, c), root, bank_a in zip(units, roots, banks_a):
+                recip = ring.tile([P, KP], F32, name="recip")
+                nc.scalar.activation(recip[:].rearrange("p (g x) -> p g x", g=PACK), root, ACT.Square)
+                if b == 0:
+                    h_bf[c] = keep.tile([P, BLOCKS * KP], BF16, name=f"h_bf{c}", tag=f"h_bf{c}", align_bytes=64)
+                nc.vector.tensor_tensor(
+                    h_bf[c][:, b * KP : (b + 1) * KP].rearrange("p (j t) -> p j t", t=PACK),
+                    bank_a[:].rearrange("p t j -> p j t"),
+                    recip[:].rearrange("p (j t) -> p j t", t=PACK),
+                    ALU.mult,
+                )
 
         def second_stage(c):
             h_codes[c] = keep.tile([P, BLOCKS * CH], U32, name=f"h_codes{c}", align_bytes=64)
@@ -216,11 +219,11 @@ def tile_list_silhouette_atlas_features_kernel(
             banks_y[c] = psum_y.tile([P, PACK, CH], F32, name="bank_y")
             for i in range(PACK):
                 for b in range(BLOCKS):
-                    scale0 = b * ROW + S + H + i * P
+                    scale0 = b * WS + H + i * P
                     nc.tensor.matmul_mx(
                         out=banks_y[c][:, i, :],
                         lhsT=wc_ord[:, b * N + i * P : b * N + (i + 1) * P].bitcast(FP8X4),
-                        lhsT_scale=plane[:, scale0 : scale0 + P],
+                        lhsT_scale=plane_w[:, scale0 : scale0 + P],
                         rhs=h_codes[c][:, b * CH : (b + 1) * CH].bitcast(FP8X4),
                         rhs_scale=h_scales[c][:, b * CH : (b + 1) * CH],
                         start=(b == 0),
@@ -228,14 +231,22 @@ def tile_list_silhouette_atlas_features_kernel(
                     )
 
         def subtract(c):
-            u, col = divmod(c * CH, HALF)
-            nc.vector.tensor_tensor(
-                diff[:, :, c * CH : (c + 1) * CH], banks_y[c][:], bd[u][:, :, col : col + CH], ALU.subtract
-            )
+            cols = slice(c * CH, (c + 1) * CH)
+            if c * CH < EARLY:
+                taken = bd_early[:, :, cols]
+            else:
+                taken = bd_late[:, :, c * CH - EARLY : (c + 1) * CH - EARLY]
+            nc.vector.tensor_tensor(diff[:, :, cols], banks_y[c][:], taken, ALU.subtract)
 
         out_rows = out.rearrange("(p i) t -> p i t", i=PACK)
 
-        pages = [keep.tile([P, T2], F32, name=f"page{i}", align_bytes=64) for i in range(PACK)]
+        pages = {}
+
+        def clear_page(i, tag, engine, pieces):
+            pages[i] = keep.tile([P, T2], F32, name=f"page{i}", tag=tag, align_bytes=64)
+            for u in range(pieces):
+                engine.memset(pages[i][:, u * T2 // pieces : (u + 1) * T2 // pieces].bitcast(I32), 0)
+
         placed = [0] * PACK
 
         def scatter(i, hi):
@@ -247,29 +258,41 @@ def tile_list_silhouette_atlas_features_kernel(
             if hi == S:
                 nc.sync.dma_start(out_rows[:, i, :], pages[i][:])
 
-        gather_words(1, 0, FIRST, "got1_lo")
-        order_wa(0)
         gather_words(1, FIRST, S, "got1_hi")
-        quantize_wb(1, 1, nc.vector.tensor_copy)
-        for c in range(AHEAD):
-            unit(0, c)
+        wc_raw = keep.tile([P, BLOCKS, N], I32, name="wc_raw", tag="wb_bf01", align_bytes=64)
+        nc.sync.dma_start(
+            wc_raw[:], wc_words.rearrange("b p c i -> b p (c i)").bitcast(I32).rearrange("b p c -> p b c")
+        )
+        quantize_wb(1, 1, nc.vector.tensor_copy, "codes11")
+
+        tail_in = keep.tile([P, (PACK + 1) * S], F32, name="tail_in", tag="ts_raw", align_bytes=64)
+        bd_early = tail_in[:, 0 : PACK * EARLY].rearrange("p (i j) -> p i j", i=PACK)
+        bd_late = tail_in[:, PACK * EARLY : PACK * S].rearrange("p (i j) -> p i j", i=PACK)
+        weight = tail_in[:, PACK * S : (PACK + 1) * S]
+        bd_rows = backdrop.rearrange("(p i) j -> p i j", i=PACK)
+        nc.sync.dma_start(bd_early, bd_rows[:, :, 0:EARLY])
+        nc.sync.dma_start(weight, wgo)
+        nc.sync.dma_start(bd_late, bd_rows[:, :, EARLY:S])
+
+        order_wa(0)
         order_wa(1)
+        unit_pair([(0, 0), (0, 1)])
         nc.vector.tensor_copy(
             wc_ord[:].bitcast(I32).rearrange("p (b i g m) -> p b g i m", b=BLOCKS, i=PACK, m=4),
             wc_raw[:].rearrange("p b (g m i) -> p b g i m", i=PACK, m=4),
         )
-        for page in pages:
-            for u in range(2):
-                nc.vector.memset(page[:, u * T2 // 2 : (u + 1) * T2 // 2].bitcast(I32), 0)
-        for c in range(CHUNKS):
-            if c >= AHEAD:
-                unit(0, c)
-            unit(1, c)
-            if c > 0:
-                subtract(c - 1)
+        for i in range(2):
+            clear_page(i, f"page{i}", nc.vector, 2)
+        unit_pair([(1, 0), (1, 1)])
+        second_stage(0)
+        for c in range(1, CHUNKS):
+            if c > 1:
+                unit_pair([(0, c), (1, c)])
+            subtract(c - 1)
             second_stage(c)
-            if c > 0:
-                scatter((c - 1) % PACK, c * CH)
+            if c <= 2:
+                clear_page(c + 1, f"h_bf{c - 1}", nc.gpsimd, 4)
+            scatter((c - 1) % PACK, c * CH)
         subtract(CHUNKS - 1)
         for i in sorted(range(PACK), key=lambda page: S - placed[page]):
             scatter(i, S)

@@ -1,6 +1,7 @@
 from contextlib import ExitStack
 
 import concourse.mybir as mybir
+from concourse.masks import make_identity
 
 K, H, N, T, S, T2 = 1024, 1024, 512, 2048, 1024, 2048
 FLOPS = 2 * K * H * S * 2 + 2 * H * N * S
@@ -29,6 +30,7 @@ QUAD = 32
 WS = H + N
 WB = PACK * KP
 FIRST = 2 * CH
+TURNED = range(PACK, CHUNKS - 1)
 RING = 4
 
 
@@ -40,8 +42,10 @@ def tile_list_silhouette_atlas_features_kernel(
         lists = ctx.enter_context(tc.tile_pool(name="lists", bufs=1))
         keep = ctx.enter_context(tc.tile_pool(name="keep", bufs=1))
         ring = ctx.enter_context(tc.tile_pool(name="ring", bufs=RING))
-        psum_ab = ctx.enter_context(tc.psum_pool(name="psum_ab", bufs=3))
-        psum_y = ctx.enter_context(tc.psum_pool(name="psum_y", bufs=2))
+        turned = ctx.enter_context(tc.tile_pool(name="turned", bufs=2))
+        psum_a = ctx.enter_context(tc.psum_pool(name="psum_a", bufs=4))
+        psum_b = ctx.enter_context(tc.psum_pool(name="psum_b", bufs=1))
+        psum_y = ctx.enter_context(tc.psum_pool(name="psum_y", bufs=1))
 
         pick = lists.tile([P, S // GROUP], U16, name="pick")
         place = lists.tile([P, S // GROUP], U16, name="place")
@@ -78,9 +82,9 @@ def tile_list_silhouette_atlas_features_kernel(
         nc.sync.dma_start(pick[:], offs)
         nc.sync.dma_start(place[:], offs2)
         load_wb(0, 0, "wb00")
-        nc.scalar.dma_start(ts_raw[0:P:4, :].bitcast(I32), tab_scales.bitcast(I32).rearrange("a q t -> q a t"))
-        nc.scalar.dma_start(ws_raw[0:P:4, 0:H].bitcast(I32), wa_scales.bitcast(I32).rearrange("a q c -> q a c"))
-        nc.scalar.dma_start(ws_raw[0:P:4, H:WS].bitcast(I32), wc_scales.bitcast(I32).rearrange("a q c -> q a c"))
+        nc.sync.dma_start(ts_raw[0:P:4, :].bitcast(I32), tab_scales.bitcast(I32).rearrange("a q t -> q a t"))
+        nc.sync.dma_start(ws_raw[0:P:4, 0:H].bitcast(I32), wa_scales.bitcast(I32).rearrange("a q c -> q a c"))
+        nc.sync.dma_start(ws_raw[0:P:4, H:WS].bitcast(I32), wc_scales.bitcast(I32).rearrange("a q c -> q a c"))
         load_wb(1, 0, "wb10")
         load_wb(0, 1, "wb01")
         load_tab(0, "tab0")
@@ -144,12 +148,14 @@ def tile_list_silhouette_atlas_features_kernel(
                 wa_raw[:].bitcast(U16).rearrange("p (a b m t) -> p b a t m", b=BLOCKS, t=PACK, m=P)[:, b],
             )
 
+        identity = keep.tile([P, P], F32, name="identity")
+        make_identity(nc, identity[:])
         h_bf, h_codes, h_scales, banks_y = {}, {}, {}, {}
         diff = keep.tile([P, PACK, S], F32, name="diff")
         wc_ord = keep.tile([P, BLOCKS * N], U32, name="wc_ord", align_bytes=64)
 
-        def product_b(b, c):
-            bank_b = psum_ab.tile([P, PACK, CH], F32, name="bank_b")
+        def product_b(b, c, side):
+            bank_b = psum_b.tile([P, PACK, CH], F32, name=f"bank_b{side}")
             for t in range(PACK):
                 for a in range(PASSES):
                     nc.tensor.matmul_mx(
@@ -164,7 +170,7 @@ def tile_list_silhouette_atlas_features_kernel(
             return bank_b
 
         def product_a(b, c):
-            bank_a = psum_ab.tile([P, PACK, CH], F32, name="bank_a")
+            bank_a = psum_a.tile([P, PACK, CH], F32, name="bank_a")
             for t in range(PACK):
                 for a in range(PASSES):
                     word0 = a * KP + t * P
@@ -181,7 +187,7 @@ def tile_list_silhouette_atlas_features_kernel(
             return bank_a
 
         def unit_pair(units):
-            banks_b = [product_b(b, c) for b, c in units]
+            banks_b = [product_b(b, c, side) for side, (b, c) in enumerate(units)]
             banks_a = [product_a(b, c) for b, c in units]
             sizes, roots = [], []
             for bank_b in banks_b:
@@ -191,7 +197,7 @@ def tile_list_silhouette_atlas_features_kernel(
                 )
                 sizes.append(size)
             for (b, c), size in zip(units, sizes):
-                if b == 1 and c > 0:
+                if b == 1 and c > 0 and c - 1 not in TURNED:
                     root = diff[:, :, (c - 1) * CH : c * CH]
                 else:
                     spare = ring.tile([P, PACK, CH], F32, name="spare")
@@ -217,6 +223,18 @@ def tile_list_silhouette_atlas_features_kernel(
             h_scales[c] = keep.tile([P, BLOCKS * CH], U8, name=f"h_scales{c}", align_bytes=64)
             nc.vector.quantize_mx(out=h_codes[c][:].bitcast(FP8X4), scales=h_scales[c][:], in_=h_bf[c][:])
             banks_y[c] = psum_y.tile([P, PACK, CH], F32, name="bank_y")
+            if c in TURNED:
+                for b in range(BLOCKS):
+                    nc.tensor.matmul_mx(
+                        out=banks_y[c][:].rearrange("p i m -> p (i m)"),
+                        lhsT=h_codes[c][:, b * CH : (b + 1) * CH].bitcast(FP8X4),
+                        lhsT_scale=h_scales[c][:, b * CH : (b + 1) * CH],
+                        rhs=wc_ord[:, b * N : (b + 1) * N].bitcast(FP8X4),
+                        rhs_scale=plane_w[:, b * WS + H : (b + 1) * WS],
+                        start=(b == 0),
+                        stop=(b == BLOCKS - 1),
+                    )
+                return
             for i in range(PACK):
                 for b in range(BLOCKS):
                     scale0 = b * WS + H + i * P
@@ -230,13 +248,36 @@ def tile_list_silhouette_atlas_features_kernel(
                         stop=(b == BLOCKS - 1),
                     )
 
-        def subtract(c):
-            cols = slice(c * CH, (c + 1) * CH)
+        def backdrop_of(c):
             if c * CH < EARLY:
-                taken = bd_early[:, :, cols]
-            else:
-                taken = bd_late[:, :, c * CH - EARLY : (c + 1) * CH - EARLY]
-            nc.vector.tensor_tensor(diff[:, :, cols], banks_y[c][:], taken, ALU.subtract)
+                return bd_early[:, :, c * CH : (c + 1) * CH]
+            return bd_late[:, :, c * CH - EARLY : (c + 1) * CH - EARLY]
+
+        minus_bd = {}
+
+        def turn_backdrop(c):
+            bank = psum_y.tile([P, PACK, P], F32, name="bank_bd")
+            for i in range(PACK):
+                nc.tensor.transpose(bank[:, i, :], backdrop_of(c)[:, i, :], identity[:])
+            minus_bd[c] = turned.tile([P, PACK, P], F32, name="minus_bd")
+            nc.scalar.activation(minus_bd[c][:], bank[:], ACT.Copy, scale=-1.0)
+
+        def subtract(c):
+            part = diff[:, :, c * CH : (c + 1) * CH]
+            if c not in TURNED:
+                nc.vector.tensor_tensor(part, banks_y[c][:], backdrop_of(c), ALU.subtract)
+                if c + 1 in TURNED:
+                    turn_backdrop(c + 1)
+                return
+            y_turned = turned.tile([P, PACK, P], F32, name="y_turned")
+            nc.scalar.copy(y_turned[:], banks_y[c][:])
+            bank = psum_y.tile([P, PACK, CH], F32, name="bank_y")
+            for i in range(PACK):
+                nc.tensor.matmul(bank[:, i, :], minus_bd[c][:, i, :], identity[:], is_transpose=True, start=True, stop=False)
+                nc.tensor.matmul(bank[:, i, :], y_turned[:, i, :], identity[:], is_transpose=True, start=False, stop=True)
+            if c + 1 in TURNED:
+                turn_backdrop(c + 1)
+            nc.scalar.copy(part, bank[:])
 
         out_rows = out.rearrange("(p i) t -> p i t", i=PACK)
 
@@ -258,14 +299,14 @@ def tile_list_silhouette_atlas_features_kernel(
             if hi == S:
                 nc.sync.dma_start(out_rows[:, i, :], pages[i][:])
 
-        gather_words(1, FIRST, S, "got1_hi")
+        gather_words(1, FIRST, 2 * FIRST, "got1_mid")
         wc_raw = keep.tile([P, BLOCKS, N], I32, name="wc_raw", tag="wb_bf01", align_bytes=64)
         nc.sync.dma_start(
             wc_raw[:], wc_words.rearrange("b p c i -> b p (c i)").bitcast(I32).rearrange("b p c -> p b c")
         )
         quantize_wb(1, 1, nc.vector.tensor_copy, "codes11")
 
-        tail_in = keep.tile([P, (PACK + 1) * S], F32, name="tail_in", tag="ts_raw", align_bytes=64)
+        tail_in = keep.tile([P, (PACK + 1) * S], F32, name="tail_in", tag="ws_raw", align_bytes=64)
         bd_early = tail_in[:, 0 : PACK * EARLY].rearrange("p (i j) -> p i j", i=PACK)
         bd_late = tail_in[:, PACK * EARLY : PACK * S].rearrange("p (i j) -> p i j", i=PACK)
         weight = tail_in[:, PACK * S : (PACK + 1) * S]
@@ -281,6 +322,7 @@ def tile_list_silhouette_atlas_features_kernel(
             wc_ord[:].bitcast(I32).rearrange("p (b i g m) -> p b g i m", b=BLOCKS, i=PACK, m=4),
             wc_raw[:].rearrange("p b (g m i) -> p b g i m", i=PACK, m=4),
         )
+        gather_words(1, 2 * FIRST, S, "wb_bf11")
         for i in range(2):
             clear_page(i, f"page{i}", nc.vector, 2)
         unit_pair([(1, 0), (1, 1)])

@@ -1,7 +1,6 @@
 from contextlib import ExitStack
 
 import concourse.mybir as mybir
-from concourse.masks import make_identity
 
 K, H, N, T, S, T2 = 1024, 1024, 512, 2048, 1024, 2048
 FLOPS = 2 * K * H * S * 2 + 2 * H * N * S
@@ -30,7 +29,6 @@ QUAD = 32
 WS = H + N
 WB = PACK * KP
 FIRST = 2 * CH
-TURNED = range(PACK, CHUNKS - 1)
 RING = 4
 
 
@@ -42,10 +40,9 @@ def tile_list_silhouette_atlas_features_kernel(
         lists = ctx.enter_context(tc.tile_pool(name="lists", bufs=1))
         keep = ctx.enter_context(tc.tile_pool(name="keep", bufs=1))
         ring = ctx.enter_context(tc.tile_pool(name="ring", bufs=RING))
-        turned = ctx.enter_context(tc.tile_pool(name="turned", bufs=2))
         psum_a = ctx.enter_context(tc.psum_pool(name="psum_a", bufs=4))
         psum_b = ctx.enter_context(tc.psum_pool(name="psum_b", bufs=1))
-        psum_y = ctx.enter_context(tc.psum_pool(name="psum_y", bufs=1))
+        psum_y = ctx.enter_context(tc.psum_pool(name="psum_y", bufs=2))
 
         pick = lists.tile([P, S // GROUP], U16, name="pick")
         place = lists.tile([P, S // GROUP], U16, name="place")
@@ -140,32 +137,28 @@ def tile_list_silhouette_atlas_features_kernel(
             wa_raw[:].rearrange("p (a c) -> p a c", a=PASSES), wa_words.bitcast(I32).rearrange("a p c -> p a c")
         )
 
-        wa_ord = [keep.tile([P, PASSES * 2 * KP], U8, name=f"wa_ord{b}", align_bytes=64) for b in range(BLOCKS)]
+        def order_wa():
+            for b in range(BLOCKS):
+                nc.vector.tensor_copy(
+                    wa_ord[:, b * 2 * H : (b + 1) * 2 * H].bitcast(U16).rearrange("p (a t m) -> p a t m", t=PACK, m=P),
+                    wa_raw[:].bitcast(U16).rearrange("p (a b m t) -> p b a t m", b=BLOCKS, t=PACK, m=P)[:, b],
+                )
 
-        def order_wa(b):
-            nc.vector.tensor_copy(
-                wa_ord[b][:].bitcast(U16).rearrange("p (a t m) -> p a t m", t=PACK, m=P),
-                wa_raw[:].bitcast(U16).rearrange("p (a b m t) -> p b a t m", b=BLOCKS, t=PACK, m=P)[:, b],
-            )
-
-        identity = keep.tile([P, P], F32, name="identity")
-        make_identity(nc, identity[:])
         h_bf, h_codes, h_scales, banks_y = {}, {}, {}, {}
         diff = keep.tile([P, PACK, S], F32, name="diff")
-        wc_ord = keep.tile([P, BLOCKS * N], U32, name="wc_ord", align_bytes=64)
 
         def product_b(b, c, side):
             bank_b = psum_b.tile([P, PACK, CH], F32, name=f"bank_b{side}")
-            for t in range(PACK):
-                for a in range(PASSES):
+            for a in range(PASSES):
+                for t in range(PACK):
                     nc.tensor.matmul_mx(
                         out=bank_b[:, t, :],
                         lhsT=wb_codes[a, b][:, t * P : (t + 1) * P].bitcast(FP8X4),
                         lhsT_scale=wb_scales[a, b][:, t * P : (t + 1) * P],
                         rhs=got[a, c].bitcast(FP8X4),
                         rhs_scale=plane_v[:, a * S + c * CH : a * S + (c + 1) * CH],
-                        start=(a == 0),
-                        stop=(a == PASSES - 1),
+                        start=(a == 0 and t == 0),
+                        stop=(a == PASSES - 1 and t == PACK - 1),
                     )
             return bank_b
 
@@ -173,11 +166,11 @@ def tile_list_silhouette_atlas_features_kernel(
             bank_a = psum_a.tile([P, PACK, CH], F32, name="bank_a")
             for t in range(PACK):
                 for a in range(PASSES):
-                    word0 = a * KP + t * P
+                    word0 = b * H + a * KP + t * P
                     scale0 = a * WS + b * KP + t * P
                     nc.tensor.matmul_mx(
                         out=bank_a[:, t, :],
-                        lhsT=wa_ord[b][:, 2 * word0 : 2 * (word0 + P)].bitcast(FP4X4),
+                        lhsT=wa_ord[:, 2 * word0 : 2 * (word0 + P)].bitcast(FP4X4),
                         lhsT_scale=plane_w[:, scale0 : scale0 + P],
                         rhs=got[a, c].bitcast(FP8X4),
                         rhs_scale=plane_v[:, a * S + c * CH : a * S + (c + 1) * CH],
@@ -186,18 +179,26 @@ def tile_list_silhouette_atlas_features_kernel(
                     )
             return bank_a
 
-        def unit_pair(units):
-            banks_b = [product_b(b, c, side) for side, (b, c) in enumerate(units)]
-            banks_a = [product_a(b, c) for b, c in units]
-            sizes, roots = [], []
+        def products_b(units):
+            return [product_b(b, c, side) for side, (b, c) in enumerate(units)]
+
+        def products_a(units):
+            return [product_a(b, c) for b, c in units]
+
+        def magnitudes(banks_b):
+            sizes = []
             for bank_b in banks_b:
                 size = ring.tile([P, KP], F32, name="size")
                 nc.scalar.activation(
                     size[:].rearrange("p (j t) -> p j t", t=PACK), bank_b[:].rearrange("p t j -> p j t"), ACT.Abs
                 )
                 sizes.append(size)
+            return sizes
+
+        def inverse_roots(units, sizes):
+            roots = []
             for (b, c), size in zip(units, sizes):
-                if b == 1 and c > 0 and c - 1 not in TURNED:
+                if b == 1 and c > 0:
                     root = diff[:, :, (c - 1) * CH : c * CH]
                 else:
                     spare = ring.tile([P, PACK, CH], F32, name="spare")
@@ -206,6 +207,9 @@ def tile_list_silhouette_atlas_features_kernel(
                     root, size[:].rearrange("p (g x) -> p g x", g=PACK), ACT.Abs_reciprocal_sqrt, bias=one[:]
                 )
                 roots.append(root)
+            return roots
+
+        def divide(units, roots, banks_a):
             for (b, c), root, bank_a in zip(units, roots, banks_a):
                 recip = ring.tile([P, KP], F32, name="recip")
                 nc.scalar.activation(recip[:].rearrange("p (g x) -> p g x", g=PACK), root, ACT.Square)
@@ -218,23 +222,13 @@ def tile_list_silhouette_atlas_features_kernel(
                     ALU.mult,
                 )
 
-        def second_stage(c):
+        def quantize_h(c):
             h_codes[c] = keep.tile([P, BLOCKS * CH], U32, name=f"h_codes{c}", align_bytes=64)
             h_scales[c] = keep.tile([P, BLOCKS * CH], U8, name=f"h_scales{c}", align_bytes=64)
             nc.vector.quantize_mx(out=h_codes[c][:].bitcast(FP8X4), scales=h_scales[c][:], in_=h_bf[c][:])
+
+        def product_y(c):
             banks_y[c] = psum_y.tile([P, PACK, CH], F32, name="bank_y")
-            if c in TURNED:
-                for b in range(BLOCKS):
-                    nc.tensor.matmul_mx(
-                        out=banks_y[c][:].rearrange("p i m -> p (i m)"),
-                        lhsT=h_codes[c][:, b * CH : (b + 1) * CH].bitcast(FP8X4),
-                        lhsT_scale=h_scales[c][:, b * CH : (b + 1) * CH],
-                        rhs=wc_ord[:, b * N : (b + 1) * N].bitcast(FP8X4),
-                        rhs_scale=plane_w[:, b * WS + H : (b + 1) * WS],
-                        start=(b == 0),
-                        stop=(b == BLOCKS - 1),
-                    )
-                return
             for i in range(PACK):
                 for b in range(BLOCKS):
                     scale0 = b * WS + H + i * P
@@ -253,31 +247,8 @@ def tile_list_silhouette_atlas_features_kernel(
                 return bd_early[:, :, c * CH : (c + 1) * CH]
             return bd_late[:, :, c * CH - EARLY : (c + 1) * CH - EARLY]
 
-        minus_bd = {}
-
-        def turn_backdrop(c):
-            bank = psum_y.tile([P, PACK, P], F32, name="bank_bd")
-            for i in range(PACK):
-                nc.tensor.transpose(bank[:, i, :], backdrop_of(c)[:, i, :], identity[:])
-            minus_bd[c] = turned.tile([P, PACK, P], F32, name="minus_bd")
-            nc.scalar.activation(minus_bd[c][:], bank[:], ACT.Copy, scale=-1.0)
-
         def subtract(c):
-            part = diff[:, :, c * CH : (c + 1) * CH]
-            if c not in TURNED:
-                nc.vector.tensor_tensor(part, banks_y[c][:], backdrop_of(c), ALU.subtract)
-                if c + 1 in TURNED:
-                    turn_backdrop(c + 1)
-                return
-            y_turned = turned.tile([P, PACK, P], F32, name="y_turned")
-            nc.scalar.copy(y_turned[:], banks_y[c][:])
-            bank = psum_y.tile([P, PACK, CH], F32, name="bank_y")
-            for i in range(PACK):
-                nc.tensor.matmul(bank[:, i, :], minus_bd[c][:, i, :], identity[:], is_transpose=True, start=True, stop=False)
-                nc.tensor.matmul(bank[:, i, :], y_turned[:, i, :], identity[:], is_transpose=True, start=False, stop=True)
-            if c + 1 in TURNED:
-                turn_backdrop(c + 1)
-            nc.scalar.copy(part, bank[:])
+            nc.vector.tensor_tensor(diff[:, :, c * CH : (c + 1) * CH], banks_y[c][:], backdrop_of(c), ALU.subtract)
 
         out_rows = out.rearrange("(p i) t -> p i t", i=PACK)
 
@@ -315,25 +286,42 @@ def tile_list_silhouette_atlas_features_kernel(
         nc.sync.dma_start(weight, wgo)
         nc.sync.dma_start(bd_late, bd_rows[:, :, EARLY:S])
 
-        order_wa(0)
-        order_wa(1)
-        unit_pair([(0, 0), (0, 1)])
+        wa_ord = keep.tile([P, BLOCKS * 2 * H], U8, name="wa_ord", tag="wb_bf11", align_bytes=64)
+        order_wa()
+        pairs = [[(b, 0), (b, 1)] for b in range(BLOCKS)] + [[(0, c), (1, c)] for c in range(2, CHUNKS)]
+        banks_b = products_b(pairs[0])
+        sizes = magnitudes(banks_b)
+        banks_b = products_b(pairs[1])
+        banks_a = products_a(pairs[0])
+        divide(pairs[0], inverse_roots(pairs[0], sizes), banks_a)
+        banks_a = products_a(pairs[1])
+        wc_ord = keep.tile([P, BLOCKS * N], U32, name="wc_ord", tag="wb01", align_bytes=64)
         nc.vector.tensor_copy(
             wc_ord[:].bitcast(I32).rearrange("p (b i g m) -> p b g i m", b=BLOCKS, i=PACK, m=4),
             wc_raw[:].rearrange("p b (g m i) -> p b g i m", i=PACK, m=4),
         )
-        gather_words(1, 2 * FIRST, S, "wb_bf11")
         for i in range(2):
             clear_page(i, f"page{i}", nc.vector, 2)
-        unit_pair([(1, 0), (1, 1)])
-        second_stage(0)
         for c in range(1, CHUNKS):
-            if c > 1:
-                unit_pair([(0, c), (1, c)])
+            sizes = magnitudes(banks_b)
+            if c + 1 < CHUNKS:
+                banks_b = products_b(pairs[c + 1])
+            roots = inverse_roots(pairs[c], sizes)
+            divide(pairs[c], roots, banks_a)
+            if c + 1 < CHUNKS:
+                banks_a = products_a(pairs[c + 1])
+            if c == 1:
+                quantize_h(0)
+                product_y(0)
+                quantize_h(1)
+                product_y(1)
+                gather_words(1, 2 * FIRST, S, "h_bf0")
             subtract(c - 1)
-            second_stage(c)
+            if c > 1:
+                quantize_h(c)
+                product_y(c)
             if c <= 2:
-                clear_page(c + 1, f"h_bf{c - 1}", nc.gpsimd, 4)
+                clear_page(c + 1, f"h_bf{c}", nc.gpsimd, 4)
             scatter((c - 1) % PACK, c * CH)
         subtract(CHUNKS - 1)
         for i in sorted(range(PACK), key=lambda page: S - placed[page]):

@@ -63,6 +63,16 @@ def tile_list_silhouette_atlas_features_kernel(
         nc.scalar.activation(one[:], one_in[:], ACT.Abs_reciprocal_sqrt, bias=one_bias[:], scale=one_scale[:])
         nc.vector.memset(plane_v[:].bitcast(I32), 0)
 
+        pages = {}
+
+        def clear_page(i, tag, engine, pieces):
+            pages[i] = keep.tile([P, T2], F32, name=f"page{i}", tag=tag, align_bytes=64)
+            for u in range(pieces):
+                engine.memset(pages[i][:, u * T2 // pieces : (u + 1) * T2 // pieces].bitcast(I32), 0)
+
+        for i in range(2):
+            clear_page(i, f"page{i}", nc.vector, 1)
+
         tab = {}
         wb_raw = {}
 
@@ -76,9 +86,9 @@ def tile_list_silhouette_atlas_features_kernel(
             rows = wb[a * KP : (a + 1) * KP, b * KP : (b + 1) * KP]
             nc.sync.dma_start(wb_raw[a, b], rows.rearrange("(p j) c -> p j c", j=PACK))
 
+        load_wb(0, 0, "wb00")
         nc.sync.dma_start(pick[:], offs)
         nc.sync.dma_start(place[:], offs2)
-        load_wb(0, 0, "wb00")
         nc.sync.dma_start(ts_raw[0:P:4, :].bitcast(I32), tab_scales.bitcast(I32).rearrange("a q t -> q a t"))
         nc.sync.dma_start(ws_raw[0:P:4, 0:H].bitcast(I32), wa_scales.bitcast(I32).rearrange("a q c -> q a c"))
         nc.sync.dma_start(ws_raw[0:P:4, H:WS].bitcast(I32), wc_scales.bitcast(I32).rearrange("a q c -> q a c"))
@@ -162,8 +172,7 @@ def tile_list_silhouette_atlas_features_kernel(
                     )
             return bank_b
 
-        def product_a(b, c):
-            bank_a = psum_a.tile([P, PACK, CH], F32, name="bank_a")
+        def product_a(b, c, bank_a):
             for t in range(PACK):
                 for a in range(PASSES):
                     word0 = b * H + a * KP + t * P
@@ -183,7 +192,7 @@ def tile_list_silhouette_atlas_features_kernel(
             return [product_b(b, c, side) for side, (b, c) in enumerate(units)]
 
         def products_a(units):
-            return [product_a(b, c) for b, c in units]
+            return [product_a(b, c, psum_a.tile([P, PACK, CH], F32, name="bank_a")) for b, c in units]
 
         def magnitudes(banks_b):
             sizes = []
@@ -252,13 +261,6 @@ def tile_list_silhouette_atlas_features_kernel(
 
         out_rows = out.rearrange("(p i) t -> p i t", i=PACK)
 
-        pages = {}
-
-        def clear_page(i, tag, engine, pieces):
-            pages[i] = keep.tile([P, T2], F32, name=f"page{i}", tag=tag, align_bytes=64)
-            for u in range(pieces):
-                engine.memset(pages[i][:, u * T2 // pieces : (u + 1) * T2 // pieces].bitcast(I32), 0)
-
         placed = [0] * PACK
 
         def scatter(i, hi):
@@ -292,18 +294,21 @@ def tile_list_silhouette_atlas_features_kernel(
         banks_b = products_b(pairs[0])
         sizes = magnitudes(banks_b)
         banks_b = products_b(pairs[1])
-        banks_a = products_a(pairs[0])
-        divide(pairs[0], inverse_roots(pairs[0], sizes), banks_a)
+        roots = inverse_roots(pairs[0], sizes)
+        sizes_next = magnitudes(banks_b)
+        banks_a = [
+            product_a(b, c, psum_b.tile([P, PACK, CH], F32, name=f"bank_b{side}"))
+            for side, (b, c) in enumerate(pairs[0])
+        ]
+        divide(pairs[0], roots, banks_a)
         banks_a = products_a(pairs[1])
         wc_ord = keep.tile([P, BLOCKS * N], U32, name="wc_ord", tag="wb01", align_bytes=64)
         nc.vector.tensor_copy(
             wc_ord[:].bitcast(I32).rearrange("p (b i g m) -> p b g i m", b=BLOCKS, i=PACK, m=4),
             wc_raw[:].rearrange("p b (g m i) -> p b g i m", i=PACK, m=4),
         )
-        for i in range(2):
-            clear_page(i, f"page{i}", nc.vector, 2)
         for c in range(1, CHUNKS):
-            sizes = magnitudes(banks_b)
+            sizes = sizes_next if c == 1 else magnitudes(banks_b)
             if c + 1 < CHUNKS:
                 banks_b = products_b(pairs[c + 1])
             roots = inverse_roots(pairs[c], sizes)
@@ -320,9 +325,10 @@ def tile_list_silhouette_atlas_features_kernel(
             if c > 1:
                 quantize_h(c)
                 product_y(c)
-            if c <= 2:
-                clear_page(c + 1, f"h_bf{c}", nc.gpsimd, 4)
-            scatter((c - 1) % PACK, c * CH)
+            if 2 <= c < PACK:
+                clear_page(c, f"h_bf{c}", nc.gpsimd, 2)
+            if c > 1:
+                scatter((c - 2) % PACK, c * CH)
         subtract(CHUNKS - 1)
         for i in sorted(range(PACK), key=lambda page: S - placed[page]):
             scatter(i, S)

@@ -40,8 +40,7 @@ def tile_list_silhouette_atlas_features_kernel(
         lists = ctx.enter_context(tc.tile_pool(name="lists", bufs=1))
         keep = ctx.enter_context(tc.tile_pool(name="keep", bufs=1))
         ring = ctx.enter_context(tc.tile_pool(name="ring", bufs=RING))
-        psum_a = ctx.enter_context(tc.psum_pool(name="psum_a", bufs=4))
-        psum_b = ctx.enter_context(tc.psum_pool(name="psum_b", bufs=1))
+        psum_ab = ctx.enter_context(tc.psum_pool(name="psum_ab", bufs=1))
         psum_y = ctx.enter_context(tc.psum_pool(name="psum_y", bufs=2))
 
         pick = lists.tile([P, S // GROUP], U16, name="pick")
@@ -50,6 +49,7 @@ def tile_list_silhouette_atlas_features_kernel(
         ts_raw = keep.tile([P, T], U8, name="ts_raw", tag="ts_raw", align_bytes=64)
         ws_raw = keep.tile([P, WS], U8, name="ws_raw", tag="ws_raw", align_bytes=64)
         plane_v = keep.tile([P, PASSES * S], U8, name="plane_v", align_bytes=64)
+        plane_w = keep.tile([P, PASSES * WS], U8, name="plane_w", align_bytes=64)
         nc.vector.memset(ts_raw[:].bitcast(I32), 0)
         nc.vector.memset(ws_raw[:].bitcast(I32), 0)
 
@@ -62,6 +62,7 @@ def tile_list_silhouette_atlas_features_kernel(
         nc.vector.memset(one_bias[:], 0.0)
         nc.scalar.activation(one[:], one_in[:], ACT.Abs_reciprocal_sqrt, bias=one_bias[:], scale=one_scale[:])
         nc.vector.memset(plane_v[:].bitcast(I32), 0)
+        nc.vector.memset(plane_w[:].bitcast(I32), 0)
 
         pages = {}
 
@@ -70,9 +71,6 @@ def tile_list_silhouette_atlas_features_kernel(
             for u in range(pieces):
                 engine.memset(pages[i][:, u * T2 // pieces : (u + 1) * T2 // pieces].bitcast(I32), 0)
 
-        for i in range(2):
-            clear_page(i, f"page{i}", nc.vector, 1)
-
         tab = {}
         wb_raw = {}
 
@@ -80,11 +78,13 @@ def tile_list_silhouette_atlas_features_kernel(
             tab[a] = keep.tile([P, T], I32, name=f"tab{a}", tag=tag, align_bytes=64)
             nc.sync.dma_start(tab[a][:], tab_words[a].rearrange("p t i -> p (t i)").bitcast(I32))
 
-        def load_wb(a, b, tag):
+        def load_wb(a, b, tag, pieces=1):
             room = keep.tile([P, WB], F32, name=f"wb{a}{b}", tag=tag, align_bytes=64)
             wb_raw[a, b] = room[:].rearrange("p (j c) -> p j c", j=PACK)
             rows = wb[a * KP : (a + 1) * KP, b * KP : (b + 1) * KP]
-            nc.sync.dma_start(wb_raw[a, b], rows.rearrange("(p j) c -> p j c", j=PACK))
+            for u in range(pieces):
+                cols = slice(u * KP // pieces, (u + 1) * KP // pieces)
+                nc.sync.dma_start(wb_raw[a, b][:, :, cols], rows.rearrange("(p j) c -> p j c", j=PACK)[:, :, cols])
 
         load_wb(0, 0, "wb00")
         nc.sync.dma_start(pick[:], offs)
@@ -93,8 +93,8 @@ def tile_list_silhouette_atlas_features_kernel(
         nc.sync.dma_start(ws_raw[0:P:4, 0:H].bitcast(I32), wa_scales.bitcast(I32).rearrange("a q c -> q a c"))
         nc.sync.dma_start(ws_raw[0:P:4, H:WS].bitcast(I32), wc_scales.bitcast(I32).rearrange("a q c -> q a c"))
         load_wb(1, 0, "wb10")
-        load_wb(0, 1, "wb01")
         load_tab(0, "tab0")
+        load_wb(0, 1, "wb01")
 
         def move_rows(plane, rows):
             for d in range(P // QUAD):
@@ -112,7 +112,8 @@ def tile_list_silhouette_atlas_features_kernel(
             ws_ord[:].rearrange("p (g t m) -> p g t m", t=PACK, m=P),
             ws_raw[:].rearrange("p (g m t) -> p g t m", t=PACK, m=P),
         )
-        load_wb(1, 1, "ws_raw")
+        load_wb(1, 1, "ws_raw", 2)
+        move_rows(plane_w, ws_ord)
 
         got = {}
 
@@ -124,21 +125,20 @@ def tile_list_silhouette_atlas_features_kernel(
 
         wb_codes, wb_scales = {}, {}
 
-        def quantize_wb(a, b, copy, tag):
+        def quantize_wb(a, b, copy, tag, pieces=1):
             rounded = keep.tile([P, WB], BF16, name=f"wb_bf{a}{b}", tag=f"wb_bf{a}{b}", align_bytes=64)
-            copy(
-                rounded[:].rearrange("p (t m j) -> p m t j", t=PACK, j=PACK),
-                wb_raw[a, b].rearrange("p j (m t) -> p m t j", t=PACK),
-            )
+            for u in range(pieces):
+                part = slice(u * P // pieces, (u + 1) * P // pieces)
+                copy(
+                    rounded[:].rearrange("p (t m j) -> p m t j", t=PACK, j=PACK)[:, part],
+                    wb_raw[a, b].rearrange("p j (m t) -> p m t j", t=PACK)[:, part],
+                )
             wb_codes[a, b] = keep.tile([P, KP], U32, name=f"wb_codes{a}{b}", tag=tag, align_bytes=64)
             wb_scales[a, b] = keep.tile([P, KP], U8, name=f"wb_scales{a}{b}", align_bytes=64)
             nc.vector.quantize_mx(out=wb_codes[a, b][:].bitcast(FP8X4), scales=wb_scales[a, b][:], in_=rounded[:])
 
         quantize_wb(0, 0, nc.scalar.copy, "codes00")
         quantize_wb(1, 0, nc.scalar.copy, "codes10")
-        plane_w = keep.tile([P, PASSES * WS], U8, name="plane_w", tag="wb_bf10", align_bytes=64)
-        nc.vector.memset(plane_w[:].bitcast(I32), 0)
-        move_rows(plane_w, ws_ord)
         gather_words(0, 0, S, "got0")
         gather_words(1, 0, FIRST, "got1_lo")
         quantize_wb(0, 1, nc.scalar.copy, "tab0")
@@ -157,8 +157,8 @@ def tile_list_silhouette_atlas_features_kernel(
         h_bf, h_codes, h_scales, banks_y = {}, {}, {}, {}
         diff = keep.tile([P, PACK, S], F32, name="diff")
 
-        def product_b(b, c, side):
-            bank_b = psum_b.tile([P, PACK, CH], F32, name=f"bank_b{side}")
+        def product_b(b, c, bank_name):
+            bank_b = psum_ab.tile([P, PACK, CH], F32, name=bank_name)
             for a in range(PASSES):
                 for t in range(PACK):
                     nc.tensor.matmul_mx(
@@ -172,7 +172,8 @@ def tile_list_silhouette_atlas_features_kernel(
                     )
             return bank_b
 
-        def product_a(b, c, bank_a):
+        def product_a(b, c, bank_name):
+            bank_a = psum_ab.tile([P, PACK, CH], F32, name=bank_name)
             for t in range(PACK):
                 for a in range(PASSES):
                     word0 = b * H + a * KP + t * P
@@ -188,11 +189,11 @@ def tile_list_silhouette_atlas_features_kernel(
                     )
             return bank_a
 
-        def products_b(units):
-            return [product_b(b, c, side) for side, (b, c) in enumerate(units)]
+        def products_b(k):
+            return [product_b(b, c, f"bank{min(k // 2, 1)}{side}") for side, (b, c) in enumerate(pairs[k])]
 
-        def products_a(units):
-            return [product_a(b, c, psum_a.tile([P, PACK, CH], F32, name="bank_a")) for b, c in units]
+        def products_a(k):
+            return [product_a(b, c, f"bank{1 if k == 0 else 2 * (k % 2)}{side}") for side, (b, c) in enumerate(pairs[k])]
 
         def magnitudes(banks_b):
             sizes = []
@@ -277,7 +278,7 @@ def tile_list_silhouette_atlas_features_kernel(
         nc.sync.dma_start(
             wc_raw[:], wc_words.rearrange("b p c i -> b p (c i)").bitcast(I32).rearrange("b p c -> p b c")
         )
-        quantize_wb(1, 1, nc.vector.tensor_copy, "codes11")
+        quantize_wb(1, 1, nc.vector.tensor_copy, "codes11", 2)
 
         tail_in = keep.tile([P, (PACK + 1) * S], F32, name="tail_in", tag="ws_raw", align_bytes=64)
         bd_early = tail_in[:, 0 : PACK * EARLY].rearrange("p (i j) -> p i j", i=PACK)
@@ -291,42 +292,37 @@ def tile_list_silhouette_atlas_features_kernel(
         wa_ord = keep.tile([P, BLOCKS * 2 * H], U8, name="wa_ord", tag="wb_bf11", align_bytes=64)
         order_wa()
         pairs = [[(b, 0), (b, 1)] for b in range(BLOCKS)] + [[(0, c), (1, c)] for c in range(2, CHUNKS)]
-        banks_b = products_b(pairs[0])
+        banks_b = products_b(0)
         sizes = magnitudes(banks_b)
-        banks_b = products_b(pairs[1])
-        roots = inverse_roots(pairs[0], sizes)
-        sizes_next = magnitudes(banks_b)
-        banks_a = [
-            product_a(b, c, psum_b.tile([P, PACK, CH], F32, name=f"bank_b{side}"))
-            for side, (b, c) in enumerate(pairs[0])
-        ]
-        divide(pairs[0], roots, banks_a)
-        banks_a = products_a(pairs[1])
+        banks_b = products_b(1)
+        banks_a = products_a(0)
+        divide(pairs[0], inverse_roots(pairs[0], sizes), banks_a)
+        banks_a = products_a(1)
         wc_ord = keep.tile([P, BLOCKS * N], U32, name="wc_ord", tag="wb01", align_bytes=64)
         nc.vector.tensor_copy(
             wc_ord[:].bitcast(I32).rearrange("p (b i g m) -> p b g i m", b=BLOCKS, i=PACK, m=4),
             wc_raw[:].rearrange("p b (g m i) -> p b g i m", i=PACK, m=4),
         )
+        gather_words(1, 2 * FIRST, S, "wb_bf01")
         for c in range(1, CHUNKS):
-            sizes = sizes_next if c == 1 else magnitudes(banks_b)
+            sizes = magnitudes(banks_b)
             if c + 1 < CHUNKS:
-                banks_b = products_b(pairs[c + 1])
+                banks_b = products_b(c + 1)
             roots = inverse_roots(pairs[c], sizes)
             divide(pairs[c], roots, banks_a)
             if c + 1 < CHUNKS:
-                banks_a = products_a(pairs[c + 1])
+                banks_a = products_a(c + 1)
             if c == 1:
                 quantize_h(0)
                 product_y(0)
                 quantize_h(1)
                 product_y(1)
-                gather_words(1, 2 * FIRST, S, "h_bf0")
             subtract(c - 1)
             if c > 1:
                 quantize_h(c)
                 product_y(c)
-            if 2 <= c < PACK:
-                clear_page(c, f"h_bf{c}", nc.gpsimd, 2)
+            if c <= PACK:
+                clear_page(c - 1, f"h_bf{c}", nc.gpsimd, 2)
             if c > 1:
                 scatter((c - 2) % PACK, c * CH)
         subtract(CHUNKS - 1)

@@ -30,6 +30,7 @@ WS = H + N
 WB = PACK * KP
 FIRST = 2 * CH
 RING = 4
+HALVES = 2
 
 
 def tile_list_silhouette_atlas_features_kernel(
@@ -64,12 +65,9 @@ def tile_list_silhouette_atlas_features_kernel(
         nc.vector.memset(plane_v[:].bitcast(I32), 0)
         nc.vector.memset(plane_w[:].bitcast(I32), 0)
 
-        pages = {}
-
-        def clear_page(i, tag, engine, pieces):
-            pages[i] = keep.tile([P, T2], F32, name=f"page{i}", tag=tag, align_bytes=64)
-            for u in range(pieces):
-                engine.memset(pages[i][:, u * T2 // pieces : (u + 1) * T2 // pieces].bitcast(I32), 0)
+        pages = [keep.tile([P, T2], F32, name=f"page{i}", align_bytes=64) for i in range(PACK)]
+        for page in pages:
+            nc.vector.memset(page[:].bitcast(I32), 0)
 
         tab = {}
         wb_raw = {}
@@ -103,7 +101,7 @@ def tile_list_silhouette_atlas_features_kernel(
                     rows[QUAD * d : QUAD * (d + 1) : 4, :].bitcast(I32),
                 )
 
-        ts_got = keep.tile([P, S], U8, name="ts_got", tag="ts_got", align_bytes=64)
+        ts_got = keep.tile([P, S], U8, name="ts_got", align_bytes=64)
         nc.vector.tensor_copy(ts_got[:], ts_raw[:].indirect(pick[:]))
         move_rows(plane_v, ts_got)
         load_tab(1, "ts_raw")
@@ -112,7 +110,7 @@ def tile_list_silhouette_atlas_features_kernel(
             ws_ord[:].rearrange("p (g t m) -> p g t m", t=PACK, m=P),
             ws_raw[:].rearrange("p (g m t) -> p g t m", t=PACK, m=P),
         )
-        load_wb(1, 1, "ws_raw", 2)
+        load_wb(1, 1, "ws_raw", HALVES)
         move_rows(plane_w, ws_ord)
 
         got = {}
@@ -189,11 +187,15 @@ def tile_list_silhouette_atlas_features_kernel(
                     )
             return bank_a
 
+        pairs = [[(b, 0), (b, 1)] for b in range(BLOCKS)] + [[(0, c), (1, c)] for c in range(2, CHUNKS)]
+
         def products_b(k):
-            return [product_b(b, c, f"bank{min(k // 2, 1)}{side}") for side, (b, c) in enumerate(pairs[k])]
+            bank_set = 0 if k < 2 else 1
+            return [product_b(b, c, f"bank{bank_set}{side}") for side, (b, c) in enumerate(pairs[k])]
 
         def products_a(k):
-            return [product_a(b, c, f"bank{1 if k == 0 else 2 * (k % 2)}{side}") for side, (b, c) in enumerate(pairs[k])]
+            bank_set = 1 if k == 0 else 2 * (k % 2)
+            return [product_a(b, c, f"bank{bank_set}{side}") for side, (b, c) in enumerate(pairs[k])]
 
         def magnitudes(banks_b):
             sizes = []
@@ -224,7 +226,7 @@ def tile_list_silhouette_atlas_features_kernel(
                 recip = ring.tile([P, KP], F32, name="recip")
                 nc.scalar.activation(recip[:].rearrange("p (g x) -> p g x", g=PACK), root, ACT.Square)
                 if b == 0:
-                    h_bf[c] = keep.tile([P, BLOCKS * KP], BF16, name=f"h_bf{c}", tag=f"h_bf{c}", align_bytes=64)
+                    h_bf[c] = keep.tile([P, BLOCKS * KP], BF16, name=f"h_bf{c}", align_bytes=64)
                 nc.vector.tensor_tensor(
                     h_bf[c][:, b * KP : (b + 1) * KP].rearrange("p (j t) -> p j t", t=PACK),
                     bank_a[:].rearrange("p t j -> p j t"),
@@ -278,7 +280,7 @@ def tile_list_silhouette_atlas_features_kernel(
         nc.sync.dma_start(
             wc_raw[:], wc_words.rearrange("b p c i -> b p (c i)").bitcast(I32).rearrange("b p c -> p b c")
         )
-        quantize_wb(1, 1, nc.vector.tensor_copy, "codes11", 2)
+        quantize_wb(1, 1, nc.vector.tensor_copy, "codes11", HALVES)
 
         tail_in = keep.tile([P, (PACK + 1) * S], F32, name="tail_in", tag="ws_raw", align_bytes=64)
         bd_early = tail_in[:, 0 : PACK * EARLY].rearrange("p (i j) -> p i j", i=PACK)
@@ -291,7 +293,6 @@ def tile_list_silhouette_atlas_features_kernel(
 
         wa_ord = keep.tile([P, BLOCKS * 2 * H], U8, name="wa_ord", tag="wb_bf11", align_bytes=64)
         order_wa()
-        pairs = [[(b, 0), (b, 1)] for b in range(BLOCKS)] + [[(0, c), (1, c)] for c in range(2, CHUNKS)]
         banks_b = products_b(0)
         sizes = magnitudes(banks_b)
         banks_b = products_b(1)
@@ -321,8 +322,6 @@ def tile_list_silhouette_atlas_features_kernel(
             if c > 1:
                 quantize_h(c)
                 product_y(c)
-            if c <= PACK:
-                clear_page(c - 1, f"h_bf{c}", nc.gpsimd, 2)
             if c > 1:
                 scatter((c - 2) % PACK, c * CH)
         subtract(CHUNKS - 1)

@@ -239,13 +239,17 @@ def tile_list_silhouette_atlas_features_kernel(
             h_scales[c] = keep.tile([P, BLOCKS * CH], U8, name=f"h_scales{c}", align_bytes=64)
             nc.vector.quantize_mx(out=h_codes[c][:].bitcast(FP8X4), scales=h_scales[c][:], in_=h_bf[c][:])
 
+        def first_page(c):
+            return (c - 1) % PACK if 2 <= c < CHUNKS - 1 else 0
+
         def product_y(c):
             banks_y[c] = psum_y.tile([P, PACK, CH], F32, name="bank_y")
-            for i in range(PACK):
+            for slot in range(PACK):
+                i = (first_page(c) + slot) % PACK
                 for b in range(BLOCKS):
                     scale0 = b * WS + H + i * P
                     nc.tensor.matmul_mx(
-                        out=banks_y[c][:, i, :],
+                        out=banks_y[c][:, slot, :],
                         lhsT=wc_ord[:, b * N + i * P : b * N + (i + 1) * P].bitcast(FP8X4),
                         lhsT_scale=plane_w[:, scale0 : scale0 + P],
                         rhs=h_codes[c][:, b * CH : (b + 1) * CH].bitcast(FP8X4),
@@ -260,7 +264,19 @@ def tile_list_silhouette_atlas_features_kernel(
             return bd_late[:, :, c * CH - EARLY : (c + 1) * CH - EARLY]
 
         def subtract(c):
-            nc.vector.tensor_tensor(diff[:, :, c * CH : (c + 1) * CH], banks_y[c][:], backdrop_of(c), ALU.subtract)
+            cols = slice(c * CH, (c + 1) * CH)
+            first = first_page(c)
+            soon = PACK if c < 2 else 1 if c < CHUNKS - 1 else 2
+            rows = slice(first, first + soon)
+            nc.vector.tensor_tensor(diff[:, rows, cols], banks_y[c][:, 0:soon, :], backdrop_of(c)[:, rows], ALU.subtract)
+            if soon == PACK:
+                return
+            late = ring.tile([P, PACK - soon, CH], F32, name="late")
+            nc.scalar.copy(late[:], banks_y[c][:, soon:PACK, :])
+            above = PACK - soon - first
+            for rows, slots in ((slice(first + soon, PACK), slice(0, above)), (slice(0, first), slice(above, PACK - soon))):
+                if rows.stop > rows.start:
+                    nc.gpsimd.tensor_tensor(diff[:, rows, cols], late[:, slots, :], backdrop_of(c)[:, rows], ALU.subtract)
 
         out_rows = out.rearrange("(p i) t -> p i t", i=PACK)
 

@@ -41,6 +41,7 @@ def tile_list_silhouette_atlas_features_kernel(
         lists = ctx.enter_context(tc.tile_pool(name="lists", bufs=1))
         keep = ctx.enter_context(tc.tile_pool(name="keep", bufs=1))
         ring = ctx.enter_context(tc.tile_pool(name="ring", bufs=RING))
+        shared = ctx.enter_context(tc.tile_pool(name="shared", bufs=1))
         psum_ab = ctx.enter_context(tc.psum_pool(name="psum_ab", bufs=1))
         psum_y = ctx.enter_context(tc.psum_pool(name="psum_y", bufs=2))
 
@@ -56,7 +57,7 @@ def tile_list_silhouette_atlas_features_kernel(
 
         one = keep.tile([P, 1], F32, name="one")
         one_in = keep.tile([P, 1], F32, name="one_in", tag="wb10", align_bytes=64)
-        one_scale = keep.tile([P, 1], F32, name="one_scale", tag="wb01", align_bytes=64)
+        one_scale = shared.tile([P, 1], F32, name="one_scale", offset=0, align_bytes=64)
         one_bias = keep.tile([P, 1], F32, name="one_bias", tag="tab0", align_bytes=64)
         nc.vector.memset(one_in[:], 1.0)
         nc.vector.memset(one_scale[:], 1.0)
@@ -77,7 +78,10 @@ def tile_list_silhouette_atlas_features_kernel(
             nc.sync.dma_start(tab[a][:], tab_words[a].rearrange("p t i -> p (t i)").bitcast(I32))
 
         def load_wb(a, b, tag, pieces=1):
-            room = keep.tile([P, WB], F32, name=f"wb{a}{b}", tag=tag, align_bytes=64)
+            if tag is None:
+                room = shared.tile([P, WB], F32, name=f"wb{a}{b}", offset=0, align_bytes=64)
+            else:
+                room = keep.tile([P, WB], F32, name=f"wb{a}{b}", tag=tag, align_bytes=64)
             wb_raw[a, b] = room[:].rearrange("p (j c) -> p j c", j=PACK)
             rows = wb[a * KP : (a + 1) * KP, b * KP : (b + 1) * KP]
             for u in range(pieces):
@@ -92,7 +96,7 @@ def tile_list_silhouette_atlas_features_kernel(
         nc.sync.dma_start(ws_raw[0:P:4, H:WS].bitcast(I32), wc_scales.bitcast(I32).rearrange("a q c -> q a c"))
         load_wb(1, 0, "wb10")
         load_tab(0, "tab0")
-        load_wb(0, 1, "wb01")
+        load_wb(0, 1, None)
 
         def move_rows(plane, rows):
             for d in range(P // QUAD):
@@ -116,7 +120,10 @@ def tile_list_silhouette_atlas_features_kernel(
         got = {}
 
         def gather_words(a, lo, hi, tag):
-            words = keep.tile([P, hi - lo], U32, name=f"got{a}_{lo}", tag=tag, align_bytes=64)
+            if tag is None:
+                words = shared.tile([P, hi - lo], U32, name=f"got{a}_{lo}", offset=2 * WB, align_bytes=64)
+            else:
+                words = keep.tile([P, hi - lo], U32, name=f"got{a}_{lo}", tag=tag, align_bytes=64)
             nc.vector.tensor_copy(words[:], tab[a][:].bitcast(U32).indirect(pick[:, lo // GROUP : hi // GROUP]))
             for c in range(lo // CH, hi // CH):
                 got[a, c] = words[:, c * CH - lo : (c + 1) * CH - lo]
@@ -140,7 +147,7 @@ def tile_list_silhouette_atlas_features_kernel(
         gather_words(0, 0, S, "got0")
         gather_words(1, 0, FIRST, "got1_lo")
         quantize_wb(0, 1, nc.scalar.copy, "tab0")
-        wa_raw = keep.tile([P, H], I32, name="wa_raw", tag="wb01", align_bytes=64)
+        wa_raw = shared.tile([P, H], I32, name="wa_raw", offset=WB, align_bytes=64)
         nc.sync.dma_start(
             wa_raw[:].rearrange("p (a c) -> p a c", a=PASSES), wa_words.bitcast(I32).rearrange("a p c -> p a c")
         )
@@ -240,7 +247,7 @@ def tile_list_silhouette_atlas_features_kernel(
             nc.vector.quantize_mx(out=h_codes[c][:].bitcast(FP8X4), scales=h_scales[c][:], in_=h_bf[c][:])
 
         def first_page(c):
-            return (c - 1) % PACK if 2 <= c < CHUNKS - 1 else 0
+            return c % PACK if 2 <= c < CHUNKS - 2 else 1 if c == CHUNKS - 2 else 0
 
         def product_y(c):
             banks_y[c] = psum_y.tile([P, PACK, CH], F32, name="bank_y")
@@ -266,7 +273,7 @@ def tile_list_silhouette_atlas_features_kernel(
         def subtract(c):
             cols = slice(c * CH, (c + 1) * CH)
             first = first_page(c)
-            soon = PACK if c < 2 else 1 if c < CHUNKS - 1 else 2
+            soon = PACK if c < 2 or c == CHUNKS - 1 else 2 if c == CHUNKS - 2 else 1
             rows = slice(first, first + soon)
             nc.vector.tensor_tensor(diff[:, rows, cols], banks_y[c][:, 0:soon, :], backdrop_of(c)[:, rows], ALU.subtract)
             if soon == PACK:
@@ -289,7 +296,8 @@ def tile_list_silhouette_atlas_features_kernel(
             )
             placed[i] = hi
             if hi == S:
-                nc.sync.dma_start(out_rows[:, i, :], pages[i][:])
+                nc.sync.dma_start(out_rows[:, i, 0 : T2 // 2], pages[i][:, 0 : T2 // 2])
+                nc.scalar.dma_start(out_rows[:, i, T2 // 2 : T2], pages[i][:, T2 // 2 : T2])
 
         gather_words(1, FIRST, 2 * FIRST, "got1_mid")
         wc_raw = keep.tile([P, BLOCKS, N], I32, name="wc_raw", tag="wb_bf01", align_bytes=64)
@@ -315,12 +323,13 @@ def tile_list_silhouette_atlas_features_kernel(
         banks_a = products_a(0)
         divide(pairs[0], inverse_roots(pairs[0], sizes), banks_a)
         banks_a = products_a(1)
-        wc_ord = keep.tile([P, BLOCKS * N], U32, name="wc_ord", tag="wb01", align_bytes=64)
-        nc.vector.tensor_copy(
-            wc_ord[:].bitcast(I32).rearrange("p (b i g m) -> p b g i m", b=BLOCKS, i=PACK, m=4),
-            wc_raw[:].rearrange("p b (g m i) -> p b g i m", i=PACK, m=4),
-        )
-        gather_words(1, 2 * FIRST, S, "wb_bf01")
+        wc_ord = shared.tile([P, BLOCKS * N], U32, name="wc_ord", offset=0, align_bytes=64)
+        for b in range(BLOCKS):
+            nc.gpsimd.tensor_copy(
+                wc_ord[:, b * N : (b + 1) * N].bitcast(I32).rearrange("p (i m) -> p i m", i=PACK),
+                wc_raw[:, b, :].rearrange("p (m i) -> p i m", i=PACK),
+            )
+        gather_words(1, 2 * FIRST, S, None)
         for c in range(1, CHUNKS):
             sizes = magnitudes(banks_b)
             if c + 1 < CHUNKS:
@@ -338,8 +347,7 @@ def tile_list_silhouette_atlas_features_kernel(
             if c > 1:
                 quantize_h(c)
                 product_y(c)
-            if c > 1:
-                scatter((c - 2) % PACK, c * CH)
+            scatter((c - 1) % PACK, c * CH)
         subtract(CHUNKS - 1)
         for i in sorted(range(PACK), key=lambda page: S - placed[page]):
             scatter(i, S)

@@ -66,7 +66,7 @@ def tile_list_silhouette_atlas_features_kernel(
         nc.vector.memset(plane_v[:].bitcast(I32), 0)
         nc.vector.memset(plane_w[:].bitcast(I32), 0)
 
-        pages = [keep.tile([P, T2], F32, name=f"page{i}", align_bytes=64) for i in range(PACK)]
+        pages = [keep.tile([P, T2], F32, name=f"page{i}", align_bytes=64) for i in range(PACK - 1)]
         for page in pages:
             nc.vector.memset(page[:].bitcast(I32), 0)
 
@@ -143,8 +143,10 @@ def tile_list_silhouette_atlas_features_kernel(
             nc.vector.quantize_mx(out=wb_codes[a, b][:].bitcast(FP8X4), scales=wb_scales[a, b][:], in_=rounded[:])
 
         quantize_wb(0, 0, nc.scalar.copy, "codes00")
-        quantize_wb(1, 0, nc.scalar.copy, "codes10")
+        pages.append(keep.tile([P, T2], F32, name="page3", tag="wb_bf00", align_bytes=64))
+        nc.gpsimd.memset(pages[PACK - 1][:].bitcast(I32), 0)
         gather_words(0, 0, S, "got0")
+        quantize_wb(1, 0, nc.scalar.copy, "codes10")
         gather_words(1, 0, FIRST, "got1_lo")
         quantize_wb(0, 1, nc.scalar.copy, "tab0")
         wa_raw = shared.tile([P, H], I32, name="wa_raw", offset=WB, align_bytes=64)

@@ -248,8 +248,10 @@ def tile_list_silhouette_atlas_features_kernel(
             h_scales[c] = keep.tile([P, BLOCKS * CH], U8, name=f"h_scales{c}", align_bytes=64)
             nc.vector.quantize_mx(out=h_codes[c][:].bitcast(FP8X4), scales=h_scales[c][:], in_=h_bf[c][:])
 
+        turns = [0, 1, 3, 2, 0, 1, 0]
+
         def first_page(c):
-            return c % PACK if 2 <= c < CHUNKS - 2 else 1 if c == CHUNKS - 2 else 0
+            return turns[c] if 2 <= c < CHUNKS - 1 else 0
 
         def product_y(c):
             banks_y[c] = psum_y.tile([P, PACK, CH], F32, name="bank_y")
@@ -272,20 +274,18 @@ def tile_list_silhouette_atlas_features_kernel(
                 return bd_early[:, :, c * CH : (c + 1) * CH]
             return bd_late[:, :, c * CH - EARLY : (c + 1) * CH - EARLY]
 
-        def subtract(c):
+        def subtract(c, room):
             cols = slice(c * CH, (c + 1) * CH)
             first = first_page(c)
-            soon = PACK if c < 2 or c == CHUNKS - 1 else 2 if c == CHUNKS - 2 else 1
+            soon = PACK if c < 2 or c == CHUNKS - 1 else 1
+            if soon < PACK:
+                nc.scalar.copy(room[:, soon:PACK, :], banks_y[c][:, soon:PACK, :])
             rows = slice(first, first + soon)
             nc.vector.tensor_tensor(diff[:, rows, cols], banks_y[c][:, 0:soon, :], backdrop_of(c)[:, rows], ALU.subtract)
-            if soon == PACK:
-                return
-            late = ring.tile([P, PACK - soon, CH], F32, name="late")
-            nc.scalar.copy(late[:], banks_y[c][:, soon:PACK, :])
-            above = PACK - soon - first
-            for rows, slots in ((slice(first + soon, PACK), slice(0, above)), (slice(0, first), slice(above, PACK - soon))):
+            wrap = PACK - first
+            for rows, slots in ((slice(first + soon, PACK), slice(soon, wrap)), (slice(0, first), slice(wrap, PACK))):
                 if rows.stop > rows.start:
-                    nc.gpsimd.tensor_tensor(diff[:, rows, cols], late[:, slots, :], backdrop_of(c)[:, rows], ALU.subtract)
+                    nc.gpsimd.tensor_tensor(diff[:, rows, cols], room[:, slots, :], backdrop_of(c)[:, rows], ALU.subtract)
 
         out_rows = out.rearrange("(p i) t -> p i t", i=PACK)
 
@@ -345,11 +345,11 @@ def tile_list_silhouette_atlas_features_kernel(
                 product_y(0)
                 quantize_h(1)
                 product_y(1)
-            subtract(c - 1)
+            subtract(c - 1, roots[0])
             if c > 1:
                 quantize_h(c)
                 product_y(c)
-            scatter((c - 1) % PACK, c * CH)
-        subtract(CHUNKS - 1)
+            scatter(turns[c - 1], c * CH)
+        subtract(CHUNKS - 1, None)
         for i in sorted(range(PACK), key=lambda page: S - placed[page]):
             scatter(i, S)

@@ -30,6 +30,8 @@ WS = H + N
 WB = PACK * KP
 FIRST = 2 * CH
 RING = 4
+LINE = 8
+AT_LAST = 4 * WB
 HALVES = 2
 
 
@@ -49,7 +51,7 @@ def tile_list_silhouette_atlas_features_kernel(
         place = lists.tile([P, S // GROUP], U16, name="place")
 
         ts_raw = keep.tile([P, T], U8, name="ts_raw", tag="ts_raw", align_bytes=64)
-        ws_raw = keep.tile([P, WS], U8, name="ws_raw", tag="ws_raw", align_bytes=64)
+        ws_raw = shared.tile([P, WS], U8, name="ws_raw", offset=AT_LAST, align_bytes=64)
         plane_v = keep.tile([P, PASSES * S], U8, name="plane_v", align_bytes=64)
         plane_w = keep.tile([P, PASSES * WS], U8, name="plane_w", align_bytes=64)
         nc.vector.memset(ts_raw[:].bitcast(I32), 0)
@@ -77,9 +79,9 @@ def tile_list_silhouette_atlas_features_kernel(
             tab[a] = keep.tile([P, T], I32, name=f"tab{a}", tag=tag, align_bytes=64)
             nc.sync.dma_start(tab[a][:], tab_words[a].rearrange("p t i -> p (t i)").bitcast(I32))
 
-        def load_wb(a, b, tag, pieces=1):
+        def load_wb(a, b, tag, pieces=1, at=0):
             if tag is None:
-                room = shared.tile([P, WB], F32, name=f"wb{a}{b}", offset=0, align_bytes=64)
+                room = shared.tile([P, WB], F32, name=f"wb{a}{b}", offset=at, align_bytes=64)
             else:
                 room = keep.tile([P, WB], F32, name=f"wb{a}{b}", tag=tag, align_bytes=64)
             wb_raw[a, b] = room[:].rearrange("p (j c) -> p j c", j=PACK)
@@ -114,14 +116,14 @@ def tile_list_silhouette_atlas_features_kernel(
             ws_ord[:].rearrange("p (g t m) -> p g t m", t=PACK, m=P),
             ws_raw[:].rearrange("p (g m t) -> p g t m", t=PACK, m=P),
         )
-        load_wb(1, 1, "ws_raw", HALVES)
+        load_wb(1, 1, None, HALVES, AT_LAST)
         move_rows(plane_w, ws_ord)
 
         got = {}
 
-        def gather_words(a, lo, hi, tag):
+        def gather_words(a, lo, hi, tag, at=0):
             if tag is None:
-                words = shared.tile([P, hi - lo], U32, name=f"got{a}_{lo}", offset=2 * WB, align_bytes=64)
+                words = shared.tile([P, hi - lo], U32, name=f"got{a}_{lo}", offset=at, align_bytes=64)
             else:
                 words = keep.tile([P, hi - lo], U32, name=f"got{a}_{lo}", tag=tag, align_bytes=64)
             nc.vector.tensor_copy(words[:], tab[a][:].bitcast(U32).indirect(pick[:, lo // GROUP : hi // GROUP]))
@@ -138,6 +140,8 @@ def tile_list_silhouette_atlas_features_kernel(
                     rounded[:].rearrange("p (t m j) -> p m t j", t=PACK, j=PACK)[:, part],
                     wb_raw[a, b].rearrange("p j (m t) -> p m t j", t=PACK)[:, part],
                 )
+            if pieces > 1:
+                gather_words(1, FIRST, 2 * FIRST, None, AT_LAST)
             wb_codes[a, b] = keep.tile([P, KP], U32, name=f"wb_codes{a}{b}", tag=tag, align_bytes=64)
             wb_scales[a, b] = keep.tile([P, KP], U8, name=f"wb_scales{a}{b}", align_bytes=64)
             nc.vector.quantize_mx(out=wb_codes[a, b][:].bitcast(FP8X4), scales=wb_scales[a, b][:], in_=rounded[:])
@@ -157,8 +161,10 @@ def tile_list_silhouette_atlas_features_kernel(
         def order_wa():
             for b in range(BLOCKS):
                 nc.vector.tensor_copy(
-                    wa_ord[:, b * 2 * H : (b + 1) * 2 * H].bitcast(U16).rearrange("p (a t m) -> p a t m", t=PACK, m=P),
-                    wa_raw[:].bitcast(U16).rearrange("p (a b m t) -> p b a t m", b=BLOCKS, t=PACK, m=P)[:, b],
+                    wa_ord[:, b * 2 * H : (b + 1) * 2 * H]
+                    .bitcast(U16)
+                    .rearrange("p (a t g e) -> p a g t e", a=PASSES, t=PACK, e=LINE),
+                    wa_raw[:].bitcast(U16).rearrange("p (a b g e t) -> p b a g t e", a=PASSES, b=BLOCKS, t=PACK, e=LINE)[:, b],
                 )
 
         h_bf, h_codes, h_scales, banks_y = {}, {}, {}, {}
@@ -280,8 +286,9 @@ def tile_list_silhouette_atlas_features_kernel(
             soon = PACK if c < 2 or c == CHUNKS - 1 else 1
             if soon < PACK:
                 nc.scalar.copy(room[:, soon:PACK, :], banks_y[c][:, soon:PACK, :])
-            rows = slice(first, first + soon)
-            nc.vector.tensor_tensor(diff[:, rows, cols], banks_y[c][:, 0:soon, :], backdrop_of(c)[:, rows], ALU.subtract)
+            for slots in (slice(0, 1), slice(1, soon)) if c in (0, CHUNKS - 1) else (slice(0, soon),):
+                rows = slice(first + slots.start, first + slots.stop)
+                nc.vector.tensor_tensor(diff[:, rows, cols], banks_y[c][:, slots, :], backdrop_of(c)[:, rows], ALU.subtract)
             wrap = PACK - first
             for rows, slots in ((slice(first + soon, PACK), slice(soon, wrap)), (slice(0, first), slice(wrap, PACK))):
                 if rows.stop > rows.start:
@@ -301,14 +308,13 @@ def tile_list_silhouette_atlas_features_kernel(
                 nc.sync.dma_start(out_rows[:, i, 0 : T2 // 2], pages[i][:, 0 : T2 // 2])
                 nc.scalar.dma_start(out_rows[:, i, T2 // 2 : T2], pages[i][:, T2 // 2 : T2])
 
-        gather_words(1, FIRST, 2 * FIRST, "got1_mid")
         wc_raw = keep.tile([P, BLOCKS, N], I32, name="wc_raw", tag="wb_bf01", align_bytes=64)
         nc.sync.dma_start(
             wc_raw[:], wc_words.rearrange("b p c i -> b p (c i)").bitcast(I32).rearrange("b p c -> p b c")
         )
         quantize_wb(1, 1, nc.vector.tensor_copy, "codes11", HALVES)
 
-        tail_in = keep.tile([P, (PACK + 1) * S], F32, name="tail_in", tag="ws_raw", align_bytes=64)
+        tail_in = shared.tile([P, (PACK + 1) * S], F32, name="tail_in", offset=AT_LAST + 4 * FIRST, align_bytes=64)
         bd_early = tail_in[:, 0 : PACK * EARLY].rearrange("p (i j) -> p i j", i=PACK)
         bd_late = tail_in[:, PACK * EARLY : PACK * S].rearrange("p (i j) -> p i j", i=PACK)
         weight = tail_in[:, PACK * S : (PACK + 1) * S]
@@ -331,7 +337,7 @@ def tile_list_silhouette_atlas_features_kernel(
                 wc_ord[:, b * N : (b + 1) * N].bitcast(I32).rearrange("p (i m) -> p i m", i=PACK),
                 wc_raw[:, b, :].rearrange("p (m i) -> p i m", i=PACK),
             )
-        gather_words(1, 2 * FIRST, S, None)
+        gather_words(1, 2 * FIRST, S, None, 2 * WB)
         for c in range(1, CHUNKS):
             sizes = magnitudes(banks_b)
             if c + 1 < CHUNKS:

@@ -64,7 +64,9 @@ def tile_list_silhouette_atlas_features_kernel(
         nc.vector.memset(one_in[:], 1.0)
         nc.vector.memset(one_scale[:], 1.0)
         nc.vector.memset(one_bias[:], 0.0)
-        nc.scalar.activation(one[:], one_in[:], ACT.Abs_reciprocal_sqrt, bias=one_bias[:], scale=one_scale[:])
+        one_sum = keep.tile([P, 1], F32, name="one_sum")
+        nc.vector.tensor_scalar(one_sum[:], one_in[:], one_scale[:], one_bias[:], ALU.mult, ALU.add)
+        nc.scalar.activation(one[:], one_sum[:], ACT.Abs_reciprocal_sqrt)
         nc.vector.memset(plane_v[:].bitcast(I32), 0)
         nc.vector.memset(plane_w[:].bitcast(I32), 0)
 
@@ -101,7 +103,7 @@ def tile_list_silhouette_atlas_features_kernel(
         load_wb(0, 1, None)
 
         def move_rows(plane, rows):
-            for d in range(P // QUAD):
+            for d in (0, 2, 1, 3):
                 nc.sync.dma_start(
                     plane[QUAD * d : QUAD * d + 4, :].bitcast(I32).rearrange("p (a c) -> p a c", a=PASSES),
                     rows[QUAD * d : QUAD * (d + 1) : 4, :].bitcast(I32),

@@ -172,8 +172,7 @@ def tile_list_silhouette_atlas_features_kernel(
         h_bf, h_codes, h_scales, banks_y = {}, {}, {}, {}
         diff = keep.tile([P, PACK, S], F32, name="diff")
 
-        def product_b(b, c, bank_name):
-            bank_b = psum_ab.tile([P, PACK, CH], F32, name=bank_name)
+        def product_b(b, c, bank_b):
             for a in range(PASSES):
                 for t in range(PACK):
                     nc.tensor.matmul_mx(
@@ -208,7 +207,10 @@ def tile_list_silhouette_atlas_features_kernel(
 
         def products_b(k):
             bank_set = 0 if k < 2 else 1
-            return [product_b(b, c, f"bank{bank_set}{side}") for side, (b, c) in enumerate(pairs[k])]
+            return [
+                product_b(b, c, psum_ab.tile([P, PACK, CH], F32, name=f"bank{bank_set}{side}"))
+                for side, (b, c) in enumerate(pairs[k])
+            ]
 
         def products_a(k):
             bank_set = 1 if k == 0 else 2 * (k % 2)
@@ -230,7 +232,7 @@ def tile_list_silhouette_atlas_features_kernel(
                 if b == 1 and c > 0:
                     root = diff[:, :, (c - 1) * CH : c * CH]
                 else:
-                    spare = ring.tile([P, PACK, CH], F32, name="spare")
+                    spare = ring.tile([P, PACK, CH], F32, name="size" if c == 2 else "spare")
                     root = spare[:]
                 nc.scalar.activation(
                     root, size[:].rearrange("p (g x) -> p g x", g=PACK), ACT.Abs_reciprocal_sqrt, bias=one[:]
@@ -330,9 +332,11 @@ def tile_list_silhouette_atlas_features_kernel(
         banks_b = products_b(0)
         sizes = magnitudes(banks_b)
         banks_b = products_b(1)
+        ahead = [product_b(0, 2, psum_y.tile([P, PACK, CH], F32, name="bank_y"))]
         banks_a = products_a(0)
         divide(pairs[0], inverse_roots(pairs[0], sizes), banks_a)
         banks_a = products_a(1)
+        ahead.append(product_b(1, 2, psum_ab.tile([P, PACK, CH], F32, name="bank11")))
         wc_ord = shared.tile([P, BLOCKS * N], U32, name="wc_ord", offset=0, align_bytes=64)
         for b in range(BLOCKS):
             nc.gpsimd.tensor_copy(
@@ -343,7 +347,7 @@ def tile_list_silhouette_atlas_features_kernel(
         for c in range(1, CHUNKS):
             sizes = magnitudes(banks_b)
             if c + 1 < CHUNKS:
-                banks_b = products_b(c + 1)
+                banks_b = ahead if c == 1 else products_b(c + 1)
             roots = inverse_roots(pairs[c], sizes)
             divide(pairs[c], roots, banks_a)
             if c + 1 < CHUNKS:

@@ -32,6 +32,8 @@ FIRST = 2 * CH
 RING = 4
 LINE = 8
 AT_LAST = 4 * WB
+COPIED = range(3, CHUNKS - 1)
+SHARED = range(4, CHUNKS)
 HALVES = 2
 
 
@@ -226,11 +228,11 @@ def tile_list_silhouette_atlas_features_kernel(
                 sizes.append(size)
             return sizes
 
-        def inverse_roots(units, sizes):
+        def inverse_roots(units, sizes, held=None):
             roots = []
             for (b, c), size in zip(units, sizes):
                 if b == 1 and c > 0:
-                    root = diff[:, :, (c - 1) * CH : c * CH]
+                    root = held
                 else:
                     spare = ring.tile([P, PACK, CH], F32, name="size" if c == 2 else "spare")
                     root = spare[:]
@@ -240,28 +242,38 @@ def tile_list_silhouette_atlas_features_kernel(
                 roots.append(root)
             return roots
 
+        def square(root):
+            recip = ring.tile([P, KP], F32, name="recip")
+            nc.scalar.activation(recip[:].rearrange("p (g x) -> p g x", g=PACK), root, ACT.Square)
+            return recip
+
+        def rows_of_h(b, c):
+            if b == 0:
+                tag = f"h_bf{c - 1 if c in (SHARED.start, CHUNKS - 1) else c}"
+                h_bf[c] = keep.tile([P, BLOCKS * KP], BF16, name=f"h_bf{c}", tag=tag, align_bytes=64)
+            return h_bf[c][:, b * KP : (b + 1) * KP]
+
+        def multiply(b, c, bank_a, recip):
+            nc.vector.tensor_tensor(
+                rows_of_h(b, c).rearrange("p (j t) -> p j t", t=PACK),
+                bank_a[:].rearrange("p t j -> p j t"),
+                recip[:].rearrange("p (j t) -> p j t", t=PACK),
+                ALU.mult,
+            )
+
         def divide(units, roots, banks_a):
             for (b, c), root, bank_a in zip(units, roots, banks_a):
-                recip = ring.tile([P, KP], F32, name="recip")
-                nc.scalar.activation(recip[:].rearrange("p (g x) -> p g x", g=PACK), root, ACT.Square)
-                if b == 0:
-                    h_bf[c] = keep.tile([P, BLOCKS * KP], BF16, name=f"h_bf{c}", align_bytes=64)
-                nc.vector.tensor_tensor(
-                    h_bf[c][:, b * KP : (b + 1) * KP].rearrange("p (j t) -> p j t", t=PACK),
-                    bank_a[:].rearrange("p t j -> p j t"),
-                    recip[:].rearrange("p (j t) -> p j t", t=PACK),
-                    ALU.mult,
-                )
+                multiply(b, c, bank_a, square(root))
 
         def quantize_h(c):
             h_codes[c] = keep.tile([P, BLOCKS * CH], U32, name=f"h_codes{c}", align_bytes=64)
             h_scales[c] = keep.tile([P, BLOCKS * CH], U8, name=f"h_scales{c}", align_bytes=64)
             nc.vector.quantize_mx(out=h_codes[c][:].bitcast(FP8X4), scales=h_scales[c][:], in_=h_bf[c][:])
 
-        turns = [0, 1, 3, 2, 0, 1, 0]
+        turns = [0, 1, 2, 3, 0, 1, 0]
 
         def first_page(c):
-            return turns[c] if 2 <= c < CHUNKS - 1 else 0
+            return turns[c] if COPIED.start <= c < CHUNKS - 1 else 0
 
         def product_y(c):
             banks_y[c] = psum_y.tile([P, PACK, CH], F32, name="bank_y")
@@ -284,17 +296,18 @@ def tile_list_silhouette_atlas_features_kernel(
                 return bd_early[:, :, c * CH : (c + 1) * CH]
             return bd_late[:, :, c * CH - EARLY : (c + 1) * CH - EARLY]
 
-        def subtract(c, room):
+        def subtract(c, slots):
+            row = (first_page(c) + slots.start) % PACK
+            rows = slice(row, row + slots.stop - slots.start)
+            nc.vector.tensor_tensor(
+                diff[:, rows, c * CH : (c + 1) * CH], banks_y[c][:, slots, :], backdrop_of(c)[:, rows], ALU.subtract
+            )
+
+        def subtract_later_rows(c, room):
             cols = slice(c * CH, (c + 1) * CH)
             first = first_page(c)
-            soon = PACK if c < 2 or c == CHUNKS - 1 else 1
-            if soon < PACK:
-                nc.scalar.copy(room[:, soon:PACK, :], banks_y[c][:, soon:PACK, :])
-            for slots in (slice(0, 1), slice(1, soon)) if c in (0, CHUNKS - 1) else (slice(0, soon),):
-                rows = slice(first + slots.start, first + slots.stop)
-                nc.vector.tensor_tensor(diff[:, rows, cols], banks_y[c][:, slots, :], backdrop_of(c)[:, rows], ALU.subtract)
             wrap = PACK - first
-            for rows, slots in ((slice(first + soon, PACK), slice(soon, wrap)), (slice(0, first), slice(wrap, PACK))):
+            for rows, slots in ((slice(first + 1, PACK), slice(1, wrap)), (slice(0, first), slice(wrap, PACK))):
                 if rows.stop > rows.start:
                     nc.gpsimd.tensor_tensor(diff[:, rows, cols], room[:, slots, :], backdrop_of(c)[:, rows], ALU.subtract)
 
@@ -302,11 +315,17 @@ def tile_list_silhouette_atlas_features_kernel(
 
         placed = [0] * PACK
 
-        def scatter(i, hi):
+        def weigh(engine, weighted, i, lo, hi):
+            at = lo - placed[i]
+            engine.tensor_tensor(weighted[:, at : at + hi - lo], diff[:, i, lo:hi], weight[:, lo:hi], ALU.mult)
+
+        def scatter(i, hi, weighted=None):
             lo = placed[i]
-            nc.vector.tensor_tensor(
-                pages[i][:].indirect(place[:, lo // GROUP : hi // GROUP]), diff[:, i, lo:hi], weight[:, lo:hi], ALU.mult
-            )
+            window = pages[i][:].indirect(place[:, lo // GROUP : hi // GROUP])
+            if weighted is None:
+                nc.vector.tensor_tensor(window, diff[:, i, lo:hi], weight[:, lo:hi], ALU.mult)
+            else:
+                nc.vector.tensor_copy(window, weighted[:, 0 : hi - lo])
             placed[i] = hi
             if hi == S:
                 nc.sync.dma_start(out_rows[:, i, 0 : T2 // 2], pages[i][:, 0 : T2 // 2])
@@ -345,11 +364,53 @@ def tile_list_silhouette_atlas_features_kernel(
             )
         gather_words(1, 2 * FIRST, S, None, 2 * WB)
         for c in range(1, CHUNKS):
+            page = turns[c - 1]
+            weighted = None
+            width = (2 * PACK - 1) * CH
+            if c == COPIED.start:
+                both = keep.tile([P, 2 * width], F32, name="weighted_first", tag=f"h_bf{c - 1}", align_bytes=64)
+                weighted = both[:, 0:width]
+                weigh(nc.gpsimd, weighted, page, placed[page], (c - 1) * CH)
+                subtract(c - 1, slice(0, PACK))
+                weigh(nc.gpsimd, both[:, width:], turns[c], placed[turns[c]], c * CH)
+            elif c == SHARED.start:
+                weighted = both[:, width:]
+            elif c in COPIED:
+                tag = f"h_bf{c - 2 if c == SHARED.start + 1 else c - 1}"
+                room = keep.tile([P, width], F32, name=f"weighted{c}", tag=tag, align_bytes=64)
+                weighted = room[:]
+                weigh(nc.gpsimd, weighted, page, placed[page], (c - 1) * CH)
             sizes = magnitudes(banks_b)
             if c + 1 < CHUNKS:
                 banks_b = ahead if c == 1 else products_b(c + 1)
-            roots = inverse_roots(pairs[c], sizes)
-            divide(pairs[c], roots, banks_a)
+            if c in COPIED:
+                last = (c - 1) * CH - placed[page]
+                held = weighted[:, last : last + KP].rearrange("p (g x) -> p g x", g=PACK)
+            else:
+                held = diff[:, :, (c - 1) * CH : c * CH]
+            if c < COPIED.start:
+                roots = inverse_roots(pairs[c], sizes, held)
+                divide(pairs[c], roots, banks_a)
+            elif c not in SHARED:
+                roots = inverse_roots(pairs[c], sizes, held)
+                multiply(0, c, banks_a[0], square(roots[0]))
+            else:
+                roots = inverse_roots(pairs[c][:1], sizes[:1])
+                a_copy = ring.tile([P, KP], F32, name="a_copy")
+                nc.scalar.copy(a_copy[:].rearrange("p (j t) -> p j t", t=PACK), banks_a[0][:].rearrange("p t j -> p j t"))
+                recip = square(roots[0])
+                nc.gpsimd.tensor_tensor(rows_of_h(0, c), a_copy[:], recip[:], ALU.mult)
+                roots = roots + inverse_roots(pairs[c][1:], sizes[1:], held)
+            if c > COPIED.start:
+                nc.scalar.copy(roots[0][:, 1:PACK, :], banks_y[c - 1][:, 1:PACK, :])
+                if c in COPIED:
+                    subtract(c - 1, slice(0, 1))
+            if c >= COPIED.start:
+                multiply(1, c, banks_a[1], square(roots[1]))
+            if c == CHUNKS - 1:
+                subtract(c - 1, slice(0, 1))
+            if c > COPIED.start:
+                subtract_later_rows(c - 1, roots[0])
             if c + 1 < CHUNKS:
                 banks_a = products_a(c + 1)
             if c == 1:
@@ -357,11 +418,17 @@ def tile_list_silhouette_atlas_features_kernel(
                 product_y(0)
                 quantize_h(1)
                 product_y(1)
-            subtract(c - 1, roots[0])
+                subtract(0, slice(0, 1))
+                subtract(0, slice(1, PACK))
+            if c == 2:
+                subtract(1, slice(0, PACK))
+            if c in COPIED:
+                weigh(nc.vector, weighted, page, (c - 1) * CH, c * CH)
             if c > 1:
                 quantize_h(c)
                 product_y(c)
-            scatter(turns[c - 1], c * CH)
-        subtract(CHUNKS - 1, None)
+            scatter(page, c * CH, weighted)
+        subtract(CHUNKS - 1, slice(0, 1))
+        subtract(CHUNKS - 1, slice(1, PACK))
         for i in sorted(range(PACK), key=lambda page: S - placed[page]):
             scatter(i, S)

from contextlib import ExitStack

import concourse.mybir as mybir

K, H, N, T, S, T2 = 1024, 1024, 512, 2048, 1024, 2048
FLOPS = 2 * K * H * S * 2 + 2 * H * N * S

F32 = mybir.dt.float32
BF16 = mybir.dt.bfloat16
I32 = mybir.dt.int32
U32 = mybir.dt.uint32
U16 = mybir.dt.uint16
U8 = mybir.dt.uint8
FP8X4 = mybir.dt.float8_e4m3fn_x4
FP4X4 = mybir.dt.float4_e2m1fn_x4
ACT = mybir.ActivationFunctionType
ALU = mybir.AluOpType

P = 128
PACK = 4
KP = P * PACK
PASSES = K // KP
BLOCKS = H // KP
CH = 128
CHUNKS = S // CH
EARLY = 2 * CH
GROUP = 16
QUAD = 32
WS = H + N
WB = PACK * KP
FIRST = 2 * CH
RING = 4
LINE = 8
AT_LAST = 4 * WB
COPIED = range(3, CHUNKS - 1)
SHARED = range(4, CHUNKS)
HALVES = 2


def tile_list_silhouette_atlas_features_kernel(
    tc, tab_words, tab_scales, offs, wa_words, wa_scales, wb, wc_words, wc_scales, backdrop, wgo, offs2, out
):
    nc = tc.nc
    with ExitStack() as ctx:
        lists = ctx.enter_context(tc.tile_pool(name="lists", bufs=1))
        keep = ctx.enter_context(tc.tile_pool(name="keep", bufs=1))
        ring = ctx.enter_context(tc.tile_pool(name="ring", bufs=RING))
        shared = ctx.enter_context(tc.tile_pool(name="shared", bufs=1))
        psum_ab = ctx.enter_context(tc.psum_pool(name="psum_ab", bufs=1))
        psum_y = ctx.enter_context(tc.psum_pool(name="psum_y", bufs=2))

        pick = lists.tile([P, S // GROUP], U16, name="pick")
        place = lists.tile([P, S // GROUP], U16, name="place")

        ts_raw = keep.tile([P, T], U8, name="ts_raw", tag="ts_raw", align_bytes=64)
        ws_raw = shared.tile([P, WS], U8, name="ws_raw", offset=AT_LAST, align_bytes=64)
        plane_v = keep.tile([P, PASSES * S], U8, name="plane_v", align_bytes=64)
        plane_w = keep.tile([P, PASSES * WS], U8, name="plane_w", align_bytes=64)
        nc.vector.memset(ts_raw[:].bitcast(I32), 0)
        nc.vector.memset(ws_raw[:].bitcast(I32), 0)

        one = keep.tile([P, 1], F32, name="one")
        one_in = keep.tile([P, 1], F32, name="one_in", tag="wb10", align_bytes=64)
        one_scale = shared.tile([P, 1], F32, name="one_scale", offset=0, align_bytes=64)
        one_bias = keep.tile([P, 1], F32, name="one_bias", tag="tab0", align_bytes=64)
        nc.vector.memset(one_in[:], 1.0)
        nc.vector.memset(one_scale[:], 1.0)
        nc.vector.memset(one_bias[:], 0.0)
        one_sum = keep.tile([P, 1], F32, name="one_sum")
        nc.vector.tensor_scalar(one_sum[:], one_in[:], one_scale[:], one_bias[:], ALU.mult, ALU.add)
        nc.scalar.activation(one[:], one_sum[:], ACT.Abs_reciprocal_sqrt)
        nc.vector.memset(plane_v[:].bitcast(I32), 0)
        nc.vector.memset(plane_w[:].bitcast(I32), 0)

        pages = [keep.tile([P, T2], F32, name=f"page{i}", align_bytes=64) for i in range(PACK - 1)]
        for page in pages:
            nc.vector.memset(page[:].bitcast(I32), 0)

        tab = {}
        wb_raw = {}

        def load_tab(a, tag):
            tab[a] = keep.tile([P, T], I32, name=f"tab{a}", tag=tag, align_bytes=64)
            nc.sync.dma_start(tab[a][:], tab_words[a].rearrange("p t i -> p (t i)").bitcast(I32))

        def load_wb(a, b, tag, pieces=1, at=0):
            if tag is None:
                room = shared.tile([P, WB], F32, name=f"wb{a}{b}", offset=at, align_bytes=64)
            else:
                room = keep.tile([P, WB], F32, name=f"wb{a}{b}", tag=tag, align_bytes=64)
            wb_raw[a, b] = room[:].rearrange("p (j c) -> p j c", j=PACK)
            rows = wb[a * KP : (a + 1) * KP, b * KP : (b + 1) * KP]
            for u in range(pieces):
                cols = slice(u * KP // pieces, (u + 1) * KP // pieces)
                nc.sync.dma_start(wb_raw[a, b][:, :, cols], rows.rearrange("(p j) c -> p j c", j=PACK)[:, :, cols])

        load_wb(0, 0, "wb00")
        nc.sync.dma_start(pick[:], offs)
        nc.sync.dma_start(place[:], offs2)
        nc.sync.dma_start(ts_raw[0:P:4, :].bitcast(I32), tab_scales.bitcast(I32).rearrange("a q t -> q a t"))
        nc.sync.dma_start(ws_raw[0:P:4, 0:H].bitcast(I32), wa_scales.bitcast(I32).rearrange("a q c -> q a c"))
        nc.sync.dma_start(ws_raw[0:P:4, H:WS].bitcast(I32), wc_scales.bitcast(I32).rearrange("a q c -> q a c"))
        load_wb(1, 0, "wb10")
        load_tab(0, "tab0")
        load_wb(0, 1, None)

        def move_rows(plane, rows):
            for d in (0, 2, 1, 3):
                nc.sync.dma_start(
                    plane[QUAD * d : QUAD * d + 4, :].bitcast(I32).rearrange("p (a c) -> p a c", a=PASSES),
                    rows[QUAD * d : QUAD * (d + 1) : 4, :].bitcast(I32),
                )

        ts_got = keep.tile([P, S], U8, name="ts_got", align_bytes=64)
        nc.vector.tensor_copy(ts_got[:], ts_raw[:].indirect(pick[:]))
        move_rows(plane_v, ts_got)
        load_tab(1, "ts_raw")
        ws_ord = keep.tile([P, WS], U8, name="ws_ord", align_bytes=64)
        nc.vector.tensor_copy(
            ws_ord[:].rearrange("p (g t m) -> p g t m", t=PACK, m=P),
            ws_raw[:].rearrange("p (g m t) -> p g t m", t=PACK, m=P),
        )
        load_wb(1, 1, None, HALVES, AT_LAST)
        move_rows(plane_w, ws_ord)

        got = {}

        def gather_words(a, lo, hi, tag, at=0):
            if tag is None:
                words = shared.tile([P, hi - lo], U32, name=f"got{a}_{lo}", offset=at, align_bytes=64)
            else:
                words = keep.tile([P, hi - lo], U32, name=f"got{a}_{lo}", tag=tag, align_bytes=64)
            nc.vector.tensor_copy(words[:], tab[a][:].bitcast(U32).indirect(pick[:, lo // GROUP : hi // GROUP]))
            for c in range(lo // CH, hi // CH):
                got[a, c] = words[:, c * CH - lo : (c + 1) * CH - lo]

        wb_codes, wb_scales = {}, {}

        def quantize_wb(a, b, copy, tag, pieces=1):
            rounded = keep.tile([P, WB], BF16, name=f"wb_bf{a}{b}", tag=f"wb_bf{a}{b}", align_bytes=64)
            for u in range(pieces):
                part = slice(u * P // pieces, (u + 1) * P // pieces)
                copy(
                    rounded[:].rearrange("p (t m j) -> p m t j", t=PACK, j=PACK)[:, part],
                    wb_raw[a, b].rearrange("p j (m t) -> p m t j", t=PACK)[:, part],
                )
            if pieces > 1:
                gather_words(1, FIRST, 2 * FIRST, None, AT_LAST)
            wb_codes[a, b] = keep.tile([P, KP], U32, name=f"wb_codes{a}{b}", tag=tag, align_bytes=64)
            wb_scales[a, b] = keep.tile([P, KP], U8, name=f"wb_scales{a}{b}", align_bytes=64)
            nc.vector.quantize_mx(out=wb_codes[a, b][:].bitcast(FP8X4), scales=wb_scales[a, b][:], in_=rounded[:])

        quantize_wb(0, 0, nc.scalar.copy, "codes00")
        pages.append(keep.tile([P, T2], F32, name="page3", tag="wb_bf00", align_bytes=64))
        nc.gpsimd.memset(pages[PACK - 1][:].bitcast(I32), 0)
        gather_words(0, 0, S, "got0")
        quantize_wb(1, 0, nc.scalar.copy, "codes10")
        gather_words(1, 0, FIRST, "got1_lo")
        quantize_wb(0, 1, nc.scalar.copy, "tab0")
        wa_raw = shared.tile([P, H], I32, name="wa_raw", offset=WB, align_bytes=64)
        nc.sync.dma_start(
            wa_raw[:].rearrange("p (a c) -> p a c", a=PASSES), wa_words.bitcast(I32).rearrange("a p c -> p a c")
        )

        def order_wa():
            for b in range(BLOCKS):
                nc.vector.tensor_copy(
                    wa_ord[:, b * 2 * H : (b + 1) * 2 * H]
                    .bitcast(U16)
                    .rearrange("p (a t g e) -> p a g t e", a=PASSES, t=PACK, e=LINE),
                    wa_raw[:].bitcast(U16).rearrange("p (a b g e t) -> p b a g t e", a=PASSES, b=BLOCKS, t=PACK, e=LINE)[:, b],
                )

        h_bf, h_codes, h_scales, banks_y = {}, {}, {}, {}
        diff = keep.tile([P, PACK, S], F32, name="diff")

        def product_b(b, c, bank_b):
            for a in range(PASSES):
                for t in range(PACK):
                    nc.tensor.matmul_mx(
                        out=bank_b[:, t, :],
                        lhsT=wb_codes[a, b][:, t * P : (t + 1) * P].bitcast(FP8X4),
                        lhsT_scale=wb_scales[a, b][:, t * P : (t + 1) * P],
                        rhs=got[a, c].bitcast(FP8X4),
                        rhs_scale=plane_v[:, a * S + c * CH : a * S + (c + 1) * CH],
                        start=(a == 0 and t == 0),
                        stop=(a == PASSES - 1 and t == PACK - 1),
                    )
            return bank_b

        def product_a(b, c, bank_name):
            bank_a = psum_ab.tile([P, PACK, CH], F32, name=bank_name)
            for t in range(PACK):
                for a in range(PASSES):
                    word0 = b * H + a * KP + t * P
                    scale0 = a * WS + b * KP + t * P
                    nc.tensor.matmul_mx(
                        out=bank_a[:, t, :],
                        lhsT=wa_ord[:, 2 * word0 : 2 * (word0 + P)].bitcast(FP4X4),
                        lhsT_scale=plane_w[:, scale0 : scale0 + P],
                        rhs=got[a, c].bitcast(FP8X4),
                        rhs_scale=plane_v[:, a * S + c * CH : a * S + (c + 1) * CH],
                        start=(a == 0),
                        stop=(a == PASSES - 1),
                    )
            return bank_a

        pairs = [[(b, 0), (b, 1)] for b in range(BLOCKS)] + [[(0, c), (1, c)] for c in range(2, CHUNKS)]

        def products_b(k):
            bank_set = 0 if k < 2 else 1
            return [
                product_b(b, c, psum_ab.tile([P, PACK, CH], F32, name=f"bank{bank_set}{side}"))
                for side, (b, c) in enumerate(pairs[k])
            ]

        def products_a(k):
            bank_set = 1 if k == 0 else 2 * (k % 2)
            return [product_a(b, c, f"bank{bank_set}{side}") for side, (b, c) in enumerate(pairs[k])]

        def magnitudes(banks_b):
            sizes = []
            for bank_b in banks_b:
                size = ring.tile([P, KP], F32, name="size")
                nc.scalar.activation(
                    size[:].rearrange("p (j t) -> p j t", t=PACK), bank_b[:].rearrange("p t j -> p j t"), ACT.Abs
                )
                sizes.append(size)
            return sizes

        def inverse_roots(units, sizes, held=None):
            roots = []
            for (b, c), size in zip(units, sizes):
                if b == 1 and c > 0:
                    root = held
                else:
                    spare = ring.tile([P, PACK, CH], F32, name="size" if c == 2 else "spare")
                    root = spare[:]
                nc.scalar.activation(
                    root, size[:].rearrange("p (g x) -> p g x", g=PACK), ACT.Abs_reciprocal_sqrt, bias=one[:]
                )
                roots.append(root)
            return roots

        def square(root):
            recip = ring.tile([P, KP], F32, name="recip")
            nc.scalar.activation(recip[:].rearrange("p (g x) -> p g x", g=PACK), root, ACT.Square)
            return recip

        def rows_of_h(b, c):
            if b == 0:
                tag = f"h_bf{c - 1 if c in (SHARED.start, CHUNKS - 1) else c}"
                h_bf[c] = keep.tile([P, BLOCKS * KP], BF16, name=f"h_bf{c}", tag=tag, align_bytes=64)
            return h_bf[c][:, b * KP : (b + 1) * KP]

        def multiply(b, c, bank_a, recip):
            nc.vector.tensor_tensor(
                rows_of_h(b, c).rearrange("p (j t) -> p j t", t=PACK),
                bank_a[:].rearrange("p t j -> p j t"),
                recip[:].rearrange("p (j t) -> p j t", t=PACK),
                ALU.mult,
            )

        def divide(units, roots, banks_a):
            for (b, c), root, bank_a in zip(units, roots, banks_a):
                multiply(b, c, bank_a, square(root))

        def quantize_h(c):
            h_codes[c] = keep.tile([P, BLOCKS * CH], U32, name=f"h_codes{c}", align_bytes=64)
            h_scales[c] = keep.tile([P, BLOCKS * CH], U8, name=f"h_scales{c}", align_bytes=64)
            nc.vector.quantize_mx(out=h_codes[c][:].bitcast(FP8X4), scales=h_scales[c][:], in_=h_bf[c][:])

        turns = [0, 1, 2, 3, 0, 1, 0]

        def first_page(c):
            return turns[c] if COPIED.start <= c < CHUNKS - 1 else 0

        def product_y(c):
            banks_y[c] = psum_y.tile([P, PACK, CH], F32, name="bank_y")
            for slot in range(PACK):
                i = (first_page(c) + slot) % PACK
                for b in range(BLOCKS):
                    scale0 = b * WS + H + i * P
                    nc.tensor.matmul_mx(
                        out=banks_y[c][:, slot, :],
                        lhsT=wc_ord[:, b * N + i * P : b * N + (i + 1) * P].bitcast(FP8X4),
                        lhsT_scale=plane_w[:, scale0 : scale0 + P],
                        rhs=h_codes[c][:, b * CH : (b + 1) * CH].bitcast(FP8X4),
                        rhs_scale=h_scales[c][:, b * CH : (b + 1) * CH],
                        start=(b == 0),
                        stop=(b == BLOCKS - 1),
                    )

        def backdrop_of(c):
            if c * CH < EARLY:
                return bd_early[:, :, c * CH : (c + 1) * CH]
            return bd_late[:, :, c * CH - EARLY : (c + 1) * CH - EARLY]

        def subtract(c, slots):
            row = (first_page(c) + slots.start) % PACK
            rows = slice(row, row + slots.stop - slots.start)
            nc.vector.tensor_tensor(
                diff[:, rows, c * CH : (c + 1) * CH], banks_y[c][:, slots, :], backdrop_of(c)[:, rows], ALU.subtract
            )

        def subtract_later_rows(c, room):
            cols = slice(c * CH, (c + 1) * CH)
            first = first_page(c)
            wrap = PACK - first
            for rows, slots in ((slice(first + 1, PACK), slice(1, wrap)), (slice(0, first), slice(wrap, PACK))):
                if rows.stop > rows.start:
                    nc.gpsimd.tensor_tensor(diff[:, rows, cols], room[:, slots, :], backdrop_of(c)[:, rows], ALU.subtract)

        out_rows = out.rearrange("(p i) t -> p i t", i=PACK)

        placed = [0] * PACK

        def weigh(engine, weighted, i, lo, hi):
            at = lo - placed[i]
            engine.tensor_tensor(weighted[:, at : at + hi - lo], diff[:, i, lo:hi], weight[:, lo:hi], ALU.mult)

        def scatter(i, hi, weighted=None):
            lo = placed[i]
            window = pages[i][:].indirect(place[:, lo // GROUP : hi // GROUP])
            if weighted is None:
                nc.vector.tensor_tensor(window, diff[:, i, lo:hi], weight[:, lo:hi], ALU.mult)
            else:
                nc.vector.tensor_copy(window, weighted[:, 0 : hi - lo])
            placed[i] = hi
            if hi == S:
                nc.sync.dma_start(out_rows[:, i, 0 : T2 // 2], pages[i][:, 0 : T2 // 2])
                nc.scalar.dma_start(out_rows[:, i, T2 // 2 : T2], pages[i][:, T2 // 2 : T2])

        wc_raw = keep.tile([P, BLOCKS, N], I32, name="wc_raw", tag="wb_bf01", align_bytes=64)
        nc.sync.dma_start(
            wc_raw[:], wc_words.rearrange("b p c i -> b p (c i)").bitcast(I32).rearrange("b p c -> p b c")
        )
        quantize_wb(1, 1, nc.vector.tensor_copy, "codes11", HALVES)

        tail_in = shared.tile([P, (PACK + 1) * S], F32, name="tail_in", offset=AT_LAST + 4 * FIRST, align_bytes=64)
        bd_early = tail_in[:, 0 : PACK * EARLY].rearrange("p (i j) -> p i j", i=PACK)
        bd_late = tail_in[:, PACK * EARLY : PACK * S].rearrange("p (i j) -> p i j", i=PACK)
        weight = tail_in[:, PACK * S : (PACK + 1) * S]
        bd_rows = backdrop.rearrange("(p i) j -> p i j", i=PACK)
        nc.sync.dma_start(bd_early, bd_rows[:, :, 0:EARLY])
        nc.sync.dma_start(weight, wgo)
        nc.sync.dma_start(bd_late, bd_rows[:, :, EARLY:S])

        wa_ord = keep.tile([P, BLOCKS * 2 * H], U8, name="wa_ord", tag="wb_bf11", align_bytes=64)
        order_wa()
        banks_b = products_b(0)
        sizes = magnitudes(banks_b)
        banks_b = products_b(1)
        ahead = [product_b(0, 2, psum_y.tile([P, PACK, CH], F32, name="bank_y"))]
        banks_a = products_a(0)
        divide(pairs[0], inverse_roots(pairs[0], sizes), banks_a)
        banks_a = products_a(1)
        ahead.append(product_b(1, 2, psum_ab.tile([P, PACK, CH], F32, name="bank11")))
        wc_ord = shared.tile([P, BLOCKS * N], U32, name="wc_ord", offset=0, align_bytes=64)
        for b in range(BLOCKS):
            nc.gpsimd.tensor_copy(
                wc_ord[:, b * N : (b + 1) * N].bitcast(I32).rearrange("p (i m) -> p i m", i=PACK),
                wc_raw[:, b, :].rearrange("p (m i) -> p i m", i=PACK),
            )
        gather_words(1, 2 * FIRST, S, None, 2 * WB)
        for c in range(1, CHUNKS):
            page = turns[c - 1]
            weighted = None
            width = (2 * PACK - 1) * CH
            if c == COPIED.start:
                both = keep.tile([P, 2 * width], F32, name="weighted_first", tag=f"h_bf{c - 1}", align_bytes=64)
                weighted = both[:, 0:width]
                weigh(nc.gpsimd, weighted, page, placed[page], (c - 1) * CH)
                subtract(c - 1, slice(0, PACK))
                weigh(nc.gpsimd, both[:, width:], turns[c], placed[turns[c]], c * CH)
            elif c == SHARED.start:
                weighted = both[:, width:]
            elif c in COPIED:
                tag = f"h_bf{c - 2 if c == SHARED.start + 1 else c - 1}"
                room = keep.tile([P, width], F32, name=f"weighted{c}", tag=tag, align_bytes=64)
                weighted = room[:]
                weigh(nc.gpsimd, weighted, page, placed[page], (c - 1) * CH)
            sizes = magnitudes(banks_b)
            if c + 1 < CHUNKS:
                banks_b = ahead if c == 1 else products_b(c + 1)
            if c in COPIED:
                last = (c - 1) * CH - placed[page]
                held = weighted[:, last : last + KP].rearrange("p (g x) -> p g x", g=PACK)
            else:
                held = diff[:, :, (c - 1) * CH : c * CH]
            if c < COPIED.start:
                roots = inverse_roots(pairs[c], sizes, held)
                divide(pairs[c], roots, banks_a)
            elif c not in SHARED:
                roots = inverse_roots(pairs[c], sizes, held)
                multiply(0, c, banks_a[0], square(roots[0]))
            else:
                roots = inverse_roots(pairs[c][:1], sizes[:1])
                a_copy = ring.tile([P, KP], F32, name="a_copy")
                nc.scalar.copy(a_copy[:].rearrange("p (j t) -> p j t", t=PACK), banks_a[0][:].rearrange("p t j -> p j t"))
                recip = square(roots[0])
                nc.gpsimd.tensor_tensor(rows_of_h(0, c), a_copy[:], recip[:], ALU.mult)
                roots = roots + inverse_roots(pairs[c][1:], sizes[1:], held)
            if c > COPIED.start:
                nc.scalar.copy(roots[0][:, 1:PACK, :], banks_y[c - 1][:, 1:PACK, :])
                if c in COPIED:
                    subtract(c - 1, slice(0, 1))
            if c >= COPIED.start:
                multiply(1, c, banks_a[1], square(roots[1]))
            if c == CHUNKS - 1:
                subtract(c - 1, slice(0, 1))
            if c > COPIED.start:
                subtract_later_rows(c - 1, roots[0])
            if c + 1 < CHUNKS:
                banks_a = products_a(c + 1)
            if c == 1:
                quantize_h(0)
                product_y(0)
                quantize_h(1)
                product_y(1)
                subtract(0, slice(0, 1))
                subtract(0, slice(1, PACK))
            if c == 2:
                subtract(1, slice(0, PACK))
            if c in COPIED:
                weigh(nc.vector, weighted, page, (c - 1) * CH, c * CH)
            if c > 1:
                quantize_h(c)
                product_y(c)
            scatter(page, c * CH, weighted)
        subtract(CHUNKS - 1, slice(0, 1))
        subtract(CHUNKS - 1, slice(1, PACK))
        for i in sorted(range(PACK), key=lambda page: S - placed[page]):
            scatter(i, S)
